import numpy as np
import ml_dtypes


def mxq(x, axis, fmt="e4m3"):
    dtype, down = {"e4m3": (ml_dtypes.float8_e4m3fn, 7), "e5m2": (ml_dtypes.float8_e5m2, 14)}[fmt]
    v = np.moveaxis(np.asarray(x, np.float32).astype(ml_dtypes.bfloat16).astype(np.float64), axis, -1)
    blocks = v.reshape(v.shape[:-1] + (-1, 32))
    amax = np.abs(blocks).max(-1, keepdims=True)
    byte = np.maximum(np.where(amax > 0, np.frexp(amax)[1] - 1 + 127, 0) - down, 1)
    scale = np.exp2(byte - 127.0)
    codes = (blocks / scale).astype(np.float32).astype(dtype).astype(np.float64)
    return np.moveaxis((codes * scale).reshape(v.shape), -1, axis)


WIDE = False


def mx_kscale(k):
    if not WIDE:
        return np.ones(k)
    levels = np.array([10, -10, 5, -5, 0])
    if k % 512:
        return np.exp2(np.random.permutation(np.resize(levels, k // 32))).repeat(32)
    a = np.empty((k // 512, 16))
    for p in range(k // 512):
        a[p, :8] = np.random.permutation(np.resize(levels, 8))
        for g in range(8):
            far = levels[np.abs(levels - a[p, g]) >= 10]
            a[p, g + 8] = far[np.random.randint(len(far))]
    return np.exp2(a.ravel()).repeat(32)


def f64(x):
    return np.asarray(x).astype(np.float64)


def striped(idx):
    return np.tile(idx.reshape(-1, 16).T, (8, 1)).astype(np.uint16)


def unstriped(offs):
    return offs[:16].T.reshape(-1).astype(np.int64)


E2M1 = np.array([0.0, 0.5, 1.0, 1.5, 2.0, 3.0, 4.0, 6.0, -0.0, -0.5, -1.0, -1.5, -2.0, -3.0, -4.0, -6.0])


def pack_weight(w, fmt):
    k, n = w.shape
    w = f64(np.asarray(w, np.float32).astype(ml_dtypes.bfloat16)).reshape(k // 32, 32, n)
    amax = np.abs(w).max(1)
    if fmt == "e4m3":
        byte = np.frexp(amax)[1] - 1 + 127 - 7
    else:
        mant, ex = np.frexp(amax / 6.0)
        byte = np.where(mant > 0.5, ex, ex - 1) + 127
    byte = np.clip(np.where(amax > 0, byte, 1), 1, 254)
    scaled = (w * np.exp2(127.0 - byte)[:, None, :]).reshape(k, n).astype(np.float32)
    by_word = np.ascontiguousarray(scaled.reshape(k // 512, 128, 4, n).transpose(0, 1, 3, 2))
    if fmt == "e4m3":
        words = by_word.astype(ml_dtypes.float8_e4m3fn).view(np.uint8)
    else:
        c = by_word.astype(ml_dtypes.float4_e2m1fn).view(np.uint8) & 0xF
        words = (c[..., 0::2] | (c[..., 1::2] << 4)).reshape(k // 512, 128, 2 * n)
    return np.ascontiguousarray(words), np.ascontiguousarray(byte.astype(np.uint8).reshape(k // 512, 16, n))


def unpack_weight(words, scales, fmt):
    g, _, n = scales.shape
    words = np.ascontiguousarray(words).reshape(g, 128, n, -1)
    if fmt == "e4m3":
        vals = words.view(ml_dtypes.float8_e4m3fn).astype(np.float64)
    else:
        nib = np.empty((g, 128, n, 4), np.uint8)
        nib[..., 0::2] = words & 0xF
        nib[..., 1::2] = words >> 4
        vals = E2M1[nib]
    vals = vals * np.repeat(np.exp2(scales.astype(np.float64) - 127.0), 8, axis=1)[..., None]
    return vals.transpose(0, 1, 3, 2).reshape(g * 512, n)


def gelu(v):
    return 0.5 * v * (1.0 + np.tanh(np.sqrt(2.0 / np.pi) * (v + 0.044715 * v**3)))


K, K2, H, N, T, T2, S, P = 1024, 512, 1024, 512, 2048, 1024, 512, 512

def setup_inputs():
    n = np.random.standard_normal
    s = mx_kscale(K)[:, None]
    s2 = mx_kscale(K2)[:, None]
    u = mx_kscale(H)[:, None]
    tab_words, tab_scales = pack_weight(n((K, T)) * s, "e4m3")
    w2_words, w2_scales = pack_weight(n((K, H)) / np.sqrt(K) / s, "e2m1")
    w4_words, w4_scales = pack_weight(n((K, N)) / np.sqrt(K) / s, "e4m3")
    return {
        "tab_words": tab_words, "tab_scales": tab_scales,
        "offs": striped(np.random.permutation(T)[:P]),
        "offs2": striped(np.random.permutation(T2)[:S]),
        "offs3": striped(np.random.permutation(T2)[:P]),
        "base": (n((K2, T2)) * s2).astype(np.float32),
        "xs": (np.round(16 * n((K2, S))) / 16 * s2).astype(np.float32),
        "w1": (n((K2, H)) / np.sqrt(K2) / s2).astype(np.float32),
        "w2_words": w2_words, "w2_scales": w2_scales,
        "gain": (2.0 * np.exp(0.3 * n(H)) * u[:, 0]).astype(np.float32),
        "w3": (n((H, N)) / np.sqrt(H) / u).astype(np.float32),
        "w4_words": w4_words, "w4_scales": w4_scales,
    }

def reference(tab_words, tab_scales, offs, offs2, offs3, base, xs, w1, w2_words, w2_scales, gain, w3, w4_words, w4_scales):
    v = unpack_weight(tab_words, tab_scales, "e4m3")[:, unstriped(offs)]
    page = f64(base).copy()
    page[:, unstriped(offs2)] = f64(xs)
    a = mxq(f64(w1), 0, "e4m3").T @ mxq(page, 0, "e4m3")
    b = unpack_weight(w2_words, w2_scales, "e2m1").T @ v
    z = np.tanh(a[:, unstriped(offs3)]) * np.tanh(b) * f64(gain)[:, None]
    w4 = unpack_weight(w4_words, w4_scales, "e4m3")
    return mxq(f64(w3), 0, "e4m3").T @ mxq(z, 0, "e4m3") + w4.T @ v

@@ -1,0 +1,303 @@
+from contextlib import ExitStack
+
+import concourse.mybir as mybir
+from concourse.masks import make_identity
+
+K, K2, H, N, T, T2, S = 1024, 512, 1024, 512, 2048, 1024, 512
+FLOPS = 2 * (K2 * H * T2 + K * H * S + H * N * S + K * N * S)
+
+F32 = mybir.dt.float32
+BF16 = mybir.dt.bfloat16
+I32 = mybir.dt.int32
+U32 = mybir.dt.uint32
+U16 = mybir.dt.uint16
+U8 = mybir.dt.uint8
+FP8X4 = mybir.dt.float8_e4m3fn_x4
+FP4X4 = mybir.dt.float4_e2m1fn_x4
+ACT = mybir.ActivationFunctionType
+MULT = mybir.AluOpType.mult
+
+P = 128
+PACK = 4
+BANK = 512
+HALF = S // 2
+
+
+def tile_list_syndrome_ring_decoder_kernel(
+    tc, tab_words, tab_scales, offs, offs2, offs3, base, xs, w1, w2_words, w2_scales, gain, w3, w4_words, w4_scales, out
+):
+    nc = tc.nc
+    with ExitStack() as ctx:
+        keep = ctx.enter_context(tc.tile_pool(name="keep", bufs=1))
+        shared = ctx.enter_context(tc.tile_pool(name="shared", bufs=1))
+        psum = ctx.enter_context(tc.psum_pool(name="psum", bufs=1))
+
+        def sb(name, shape, dtype, tag=None):
+            return keep.tile(shape, dtype, name=name, tag=tag or name, align_bytes=64)
+
+        def placed(name, shape, dtype, offset):
+            return shared.tile(shape, dtype, name=name, align_bytes=64, offset=offset)
+
+        idx_tab = keep.tile([P, S // 16], U16, name="idx_tab")
+        idx_put = keep.tile([P, S // 16], U16, name="idx_put")
+        idx_round = keep.tile([P, S // 16], U16, name="idx_round")
+
+        tab_s = sb("tab_s", [P, T], U8)
+        w2_s_raw = sb("w2_s_raw", [P, H], U8)
+        w4_s = sb("w4_s", [P, N], U8)
+        w2_s1 = sb("w2_s1", [P, H], U8)
+        v_s = [sb(f"v_s{a}", [P, S], U8) for a in range(2)]
+        gain_rows = sb("gain_rows", [P, P], F32)
+        nc.gpsimd.memset(gain_rows[:], 0.0)
+        for plane, rows in ((tab_s, tab_scales), (w2_s_raw, w2_scales), (w4_s, w4_scales)):
+            nc.gpsimd.memset(plane[:].bitcast(I32), 0)
+            for q in range(4):
+                nc.gpsimd.dma_start(
+                    out=plane[32 * q : 32 * q + 8, :].bitcast(I32), in_=rows[:, 4 * q : 4 * q + 4, :].bitcast(I32)
+                )
+        for plane in (w2_s1, v_s[1]):
+            nc.gpsimd.memset(plane[:].bitcast(I32), 0)
+        ident = sb("ident", [P, P], F32)
+        make_identity(nc, ident[:])
+
+        page = [sb(f"page{t}", [P, T2], F32) for t in range(PACK)]
+        fresh = [sb(f"fresh{t}", [P, S], F32) for t in range(PACK)]
+        w1_raw = [placed("w1_raw0", [P, PACK, BANK], F32, 0), sb("w1_raw1", [P, PACK, BANK], F32)]
+        w3_raw = [sb("w3_raw0", [P, PACK, N], F32), placed("w3_raw1", [P, PACK, N], F32, 8192)]
+        tab_w = [sb(f"tab_w{a}", [P, T], I32) for a in range(2)]
+        w2_raw = sb("w2_raw", [P, 2, 2 * H], U8)
+        w4_w = sb("w4_w", [P, 2, N], I32)
+        gains = sb("gains", [P, 2 * PACK], F32)
+
+        base_rows = base.rearrange("(p t) c -> p t c", t=PACK)
+        xs_rows = xs.rearrange("(p t) c -> p t c", t=PACK)
+        w1_rows = w1.rearrange("(p t) c -> p t c", t=PACK)
+        w3_rows = w3.rearrange("(g m t e) n -> g t m e n", g=2, t=PACK, e=4)
+
+        def load_page(t):
+            nc.sync.dma_start(out=fresh[t][:], in_=xs_rows[:, t, :])
+            nc.sync.dma_start(out=page[t][:], in_=base_rows[:, t, :])
+
+        def load_w1(g):
+            nc.sync.dma_start(out=w1_raw[g][:], in_=w1_rows[:, :, g * BANK : (g + 1) * BANK])
+
+        def load_w3(g):
+            for t in range(PACK):
+                nc.sync.dma_start(out=w3_raw[g][:, t, :], in_=w3_rows[g, t])
+
+        def load_tab(a):
+            nc.sync.dma_start(out=tab_w[a][:], in_=tab_words[a].rearrange("p c i -> p (c i)").bitcast(I32))
+
+        nc.sync.dma_start(idx_put[:], offs2)
+        load_page(0)
+        load_w1(0)
+        load_page(1)
+        load_w1(1)
+        load_page(2)
+        load_w3(0)
+        load_page(3)
+        nc.sync.dma_start(idx_tab[:], offs)
+        load_tab(0)
+        load_w3(1)
+        load_tab(1)
+        nc.sync.dma_start(out=w2_raw[:].bitcast(I32), in_=w2_words.rearrange("a p c -> p a c").bitcast(I32))
+        nc.sync.dma_start(idx_round[:], offs3)
+        for g in range(2):
+            nc.sync.dma_start(
+                out=gain_rows[PACK * g : PACK * (g + 1), :].rearrange("t (m e) -> t m e", e=4),
+                in_=gain.rearrange("(g m t e) -> g t m e", g=2, t=PACK, e=4)[g],
+            )
+        nc.sync.dma_start(out=w4_w[:], in_=w4_words.rearrange("a p c i -> p a (c i)").bitcast(I32))
+
+        def quantize(name, grouped, width, tag=None):
+            codes = sb(f"{name}_codes", [P, width], U32, tag)
+            scales = sb(f"{name}_scales", [P, width], U8)
+            nc.vector.quantize_mx(out=codes[:].bitcast(FP8X4), scales=scales[:], in_=grouped)
+            return codes, scales
+
+        pairs = [placed(f"pairs{h}", [P, 2, BANK, 2], BF16, 4096 * h) for h in range(2)]
+        w1_q = []
+        w3_bf = [sb(f"w3_bf{g}", [P, N, PACK], BF16) for g in range(2)]
+
+        def put_rounds(t):
+            nc.vector.tensor_copy(page[t][:].indirect(idx_put[:]), fresh[t][:])
+
+        def round_page(t):
+            for h in range(2):
+                nc.scalar.copy(out=pairs[h][:, t // 2, :, t % 2], in_=page[t][:, h * BANK : (h + 1) * BANK])
+
+        def prep_w1(g):
+            w1_bf = sb(f"w1_bf{g}", [P, BANK * PACK], BF16)
+            nc.scalar.copy(
+                out=w1_bf[:].rearrange("p (t m e j) -> p t m j e", t=PACK, e=4, j=PACK),
+                in_=w1_raw[g][:].rearrange("p j (m t e) -> p t m j e", t=PACK, e=4),
+            )
+            w1_q.append(quantize(f"w1_{g}", w1_bf[:], BANK))
+
+        def cast_w3(g):
+            nc.scalar.copy(
+                out=w3_bf[g][:].rearrange("p (c i) t -> p c t i", i=4),
+                in_=w3_raw[g][:].rearrange("p t (c i) -> p c t i", i=4),
+            )
+
+        put_rounds(0)
+        prep_w1(0)
+        round_page(0)
+        put_rounds(1)
+        prep_w1(1)
+        round_page(1)
+        put_rounds(2)
+        cast_w3(0)
+        round_page(2)
+        put_rounds(3)
+        round_page(3)
+        cast_w3(1)
+
+        nc.vector.tensor_copy(v_s[0][:], tab_s[:].indirect(idx_tab[:]))
+        nc.gpsimd.dma_start(out=v_s[1][0:112, :].bitcast(I32), in_=v_s[0][4:116, :].bitcast(I32))
+        w2_s = [sb("w2_s0", [P, H], U8, "fresh3"), w2_s1]
+        nc.vector.tensor_copy(
+            out=w2_s[0][:].bitcast(I32).rearrange("p (g t m) -> p g t m", g=2, t=PACK),
+            in_=w2_s_raw[:].bitcast(I32).rearrange("p (g m t) -> p g t m", g=2, t=PACK),
+        )
+        nc.gpsimd.dma_start(out=w2_s[1][0:112, :].bitcast(I32), in_=w2_s[0][4:116, :].bitcast(I32))
+
+        page_q = []
+        for h in range(2):
+            page_bf = sb(f"page_bf{h}", [P, BANK * PACK], BF16)
+            nc.vector.tensor_copy(
+                out=page_bf[:].bitcast(F32).rearrange("p (c i u) -> p c u i", i=4, u=2),
+                in_=pairs[h][:].rearrange("p u c x -> p u (c x)").bitcast(F32).rearrange("p u (c i) -> p c u i", i=4),
+            )
+            page_q.append(quantize(f"page_{h}", page_bf[:], BANK))
+
+        v_w = [sb(f"v_w{a}", [P, S], I32) for a in range(2)]
+        w3_q = []
+        for a in range(2):
+            nc.vector.tensor_copy(v_w[a][:].bitcast(U32), tab_w[a][:].bitcast(U32).indirect(idx_tab[:]))
+            w3_q.append(quantize(f"w3_{a}", w3_bf[a][:].rearrange("p c t -> p (c t)"), N, f"page_bf{1 - a}"))
+        w2_w = sb("w2_w", [P, 2, 2 * H], U8)
+        nc.vector.tensor_copy(
+            out=w2_w[:].rearrange("p a c -> p (a c)").bitcast(I32).rearrange("p (b t m x) -> p b t m x", b=4, t=PACK, x=2),
+            in_=w2_raw[:].rearrange("p a c -> p (a c)").bitcast(I32).rearrange("p (b m t x) -> p b t m x", b=4, t=PACK, x=2),
+        )
+
+        gain_turned = psum.tile([P, BANK], F32, name="gain_turned", tag="bank3")
+        nc.tensor.transpose(gain_turned[:, 0:P], gain_rows[:], ident[:])
+        nc.scalar.copy(out=gains[:], in_=gain_turned[:, 0 : 2 * PACK])
+
+        picked = [sb(f"picked{g}", [P, PACK, S], F32) for g in range(2)]
+        hist = [sb(f"hist{g}", [P, PACK, S], F32) for g in range(2)]
+
+        def project_page(g, t):
+            if g == 0 and t < 2:
+                window = placed(f"rounds{g}{t}", [P, T2], F32, 8192 + 4096 * t)
+            else:
+                window = sb(f"rounds{g}{t}", [P, T2], F32)
+            cols = slice(t * P, (t + 1) * P)
+            for h in range(2):
+                acc = psum.tile([P, BANK], F32, name="acc", tag="acc", bufs=4)
+                nc.tensor.matmul_mx(
+                    out=acc[:],
+                    lhsT=w1_q[g][0][:, cols].bitcast(FP8X4),
+                    lhsT_scale=w1_q[g][1][:, cols],
+                    rhs=page_q[h][0][:].bitcast(FP8X4),
+                    rhs_scale=page_q[h][1][:],
+                    start=True,
+                    stop=True,
+                )
+                nc.scalar.copy(out=window[:, h * BANK : (h + 1) * BANK], in_=acc[:])
+            nc.vector.tensor_copy(picked[g][:, t, :], window[:].indirect(idx_round[:]))
+
+        def tanh_picked(g, t):
+            nc.scalar.activation(out=picked[g][:, t, :], in_=picked[g][:, t, :], func=ACT.Tanh)
+
+        def project_history(g, t):
+            acc = psum.tile([P, BANK], F32, name=f"hist_acc{g}{t}", tag=f"bank{t}")
+            c0 = g * BANK + t * P
+            for a in range(2):
+                nc.tensor.matmul_mx(
+                    out=acc[:],
+                    lhsT=w2_w[:, a, 2 * c0 : 2 * (c0 + P)].bitcast(FP4X4),
+                    lhsT_scale=w2_s[a][:, c0 : c0 + P],
+                    rhs=v_w[a][:].bitcast(FP8X4),
+                    rhs_scale=v_s[a][:],
+                    start=(a == 0),
+                    stop=(a == 1),
+                )
+            nc.scalar.activation(out=hist[g][:, t, :], in_=acc[:], func=ACT.Tanh)
+            nc.vector.tensor_scalar(
+                hist[g][:, t, :], hist[g][:, t, :], gains[:, PACK * g + t : PACK * g + t + 1], None, MULT
+            )
+
+        def messages(g, c0, c1):
+            z_bf = sb(f"z_bf{g}_{c0}", [P, c1 - c0, PACK], BF16)
+            nc.vector.tensor_tensor(
+                z_bf[:].rearrange("p (c i) t -> p c t i", i=4),
+                picked[g][:, :, c0:c1].rearrange("p t (c i) -> p c t i", i=4),
+                hist[g][:, :, c0:c1].rearrange("p t (c i) -> p c t i", i=4),
+                MULT,
+            )
+            return quantize(f"z_{g}_{c0}", z_bf[:].rearrange("p c t -> p (c t)"), c1 - c0)
+
+        def open_out(h):
+            accs = []
+            for n in range(4):
+                if h == 0:
+                    acc = psum.tile([P, BANK], F32, name=f"out_acc{h}{n}", tag="acc", bufs=4)
+                else:
+                    acc = psum.tile([P, BANK], F32, name=f"out_acc{h}{n}", tag=f"bank{n}")
+                accs.append(acc)
+                cols = slice(n * P, (n + 1) * P)
+                for a in range(2):
+                    nc.tensor.matmul_mx(
+                        out=acc[:, 0:HALF],
+                        lhsT=w4_w[:, a, cols].bitcast(FP8X4),
+                        lhsT_scale=w4_s[4 * a : P, cols],
+                        rhs=v_w[a][:, h * HALF : (h + 1) * HALF].bitcast(FP8X4),
+                        rhs_scale=v_s[a][:, h * HALF : (h + 1) * HALF],
+                        start=(a == 0),
+                        stop=False,
+                    )
+            return accs
+
+        def mix(accs, g, z, c0):
+            for n in range(4):
+                cols = slice(n * P, (n + 1) * P)
+                nc.tensor.matmul_mx(
+                    out=accs[n][:, 0:HALF],
+                    lhsT=w3_q[g][0][:, cols].bitcast(FP8X4),
+                    lhsT_scale=w3_q[g][1][:, cols],
+                    rhs=z[0][:, c0 : c0 + HALF].bitcast(FP8X4),
+                    rhs_scale=z[1][:, c0 : c0 + HALF],
+                    start=False,
+                    stop=(g == 1),
+                )
+
+        for g in range(2):
+            for t in range(PACK):
+                project_page(g, t)
+        for t in range(PACK):
+            project_history(0, t)
+        for t in range(PACK):
+            tanh_picked(0, t)
+        outs = [open_out(0)]
+        for t in range(PACK):
+            project_history(1, t)
+        z0 = messages(0, 0, S)
+        outs.append(open_out(1))
+        for h in range(2):
+            mix(outs[h], 0, z0, h * HALF)
+        for t in range(PACK):
+            tanh_picked(1, t)
+        out_rows = out.rearrange("(n p) c -> p n c", p=P)
+        for h in range(2):
+            mix(outs[h], 1, messages(1, h * HALF, (h + 1) * HALF), 0)
+            for u in range(2):
+                res = sb(f"res{h}{u}", [P, 2, HALF], F32)
+                for i in range(2):
+                    if h == 1 and u == 1:
+                        nc.vector.tensor_copy(out=res[:, i, :], in_=outs[h][2 * u + i][:, 0:HALF])
+                    else:
+                        nc.scalar.copy(out=res[:, i, :], in_=outs[h][2 * u + i][:, 0:HALF])
+                nc.sync.dma_start(out=out_rows[:, 2 * u : 2 * u + 2, h * HALF : (h + 1) * HALF], in_=res[:])

@@ -43,22 +43,22 @@ def tile_list_syndrome_ring_decoder_kernel(
         idx_round = keep.tile([P, S // 16], U16, name="idx_round")
 
         tab_s = sb("tab_s", [P, T], U8)
-        w2_s_raw = sb("w2_s_raw", [P, H], U8)
-        w4_s = sb("w4_s", [P, N], U8)
-        w2_s1 = sb("w2_s1", [P, H], U8)
+        w2_s_raw = sb("w2_s_raw", [P, 2, H], U8)
+        w4_s = sb("w4_s", [P, 2, N], U8)
         v_s = [sb(f"v_s{a}", [P, S], U8) for a in range(2)]
         gain_rows = sb("gain_rows", [P, P], F32)
-        nc.gpsimd.memset(gain_rows[:], 0.0)
-        for plane, rows in ((tab_s, tab_scales), (w2_s_raw, w2_scales), (w4_s, w4_scales)):
-            nc.gpsimd.memset(plane[:].bitcast(I32), 0)
-            for q in range(4):
-                nc.gpsimd.dma_start(
-                    out=plane[32 * q : 32 * q + 8, :].bitcast(I32), in_=rows[:, 4 * q : 4 * q + 4, :].bitcast(I32)
-                )
-        for plane in (w2_s1, v_s[1]):
-            nc.gpsimd.memset(plane[:].bitcast(I32), 0)
+        for plane in (tab_s, w2_s_raw, w4_s, v_s[1]):
+            nc.vector.memset(plane[:].bitcast(I32), 0)
+        nc.vector.memset(gain_rows[:], 0.0)
         ident = sb("ident", [P, P], F32)
         make_identity(nc, ident[:])
+
+        def load_scale_rows(planes, rows):
+            for r in range(4):
+                nc.sync.dma_start(
+                    out=planes[r:P:32, :, :].bitcast(I32),
+                    in_=rows.rearrange("a (q r) c -> r q a c", r=4)[r].bitcast(I32),
+                )
 
         page = [sb(f"page{t}", [P, T2], F32) for t in range(PACK)]
         fresh = [sb(f"fresh{t}", [P, S], F32) for t in range(PACK)]
@@ -97,8 +97,13 @@ def tile_list_syndrome_ring_decoder_kernel(
         load_w3(0)
         load_page(3)
         nc.sync.dma_start(idx_tab[:], offs)
+        for q in range(4):
+            nc.sync.dma_start(
+                out=tab_s[32 * q : 32 * q + 8, :].bitcast(I32), in_=tab_scales[:, 4 * q : 4 * q + 4, :].bitcast(I32)
+            )
         load_tab(0)
         load_w3(1)
+        load_scale_rows(w2_s_raw, w2_scales)
         load_tab(1)
         nc.sync.dma_start(out=w2_raw[:].bitcast(I32), in_=w2_words.rearrange("a p c -> p a c").bitcast(I32))
         nc.sync.dma_start(idx_round[:], offs3)
@@ -108,6 +113,7 @@ def tile_list_syndrome_ring_decoder_kernel(
                 in_=gain.rearrange("(g m t e) -> g t m e", g=2, t=PACK, e=4)[g],
             )
         nc.sync.dma_start(out=w4_w[:], in_=w4_words.rearrange("a p c i -> p a (c i)").bitcast(I32))
+        load_scale_rows(w4_s, w4_scales)
 
         def quantize(name, grouped, width, tag=None):
             codes = sb(f"{name}_codes", [P, width], U32, tag)
@@ -154,13 +160,7 @@ def tile_list_syndrome_ring_decoder_kernel(
         cast_w3(1)
 
         nc.vector.tensor_copy(v_s[0][:], tab_s[:].indirect(idx_tab[:]))
-        nc.gpsimd.dma_start(out=v_s[1][0:112, :].bitcast(I32), in_=v_s[0][4:116, :].bitcast(I32))
-        w2_s = [sb("w2_s0", [P, H], U8, "fresh3"), w2_s1]
-        nc.vector.tensor_copy(
-            out=w2_s[0][:].bitcast(I32).rearrange("p (g t m) -> p g t m", g=2, t=PACK),
-            in_=w2_s_raw[:].bitcast(I32).rearrange("p (g m t) -> p g t m", g=2, t=PACK),
-        )
-        nc.gpsimd.dma_start(out=w2_s[1][0:112, :].bitcast(I32), in_=w2_s[0][4:116, :].bitcast(I32))
+        nc.sync.dma_start(out=v_s[1][0:112, :].bitcast(I32), in_=v_s[0][4:116, :].bitcast(I32))
 
         page_q = []
         for h in range(2):
@@ -180,6 +180,12 @@ def tile_list_syndrome_ring_decoder_kernel(
         nc.vector.tensor_copy(
             out=w2_w[:].rearrange("p a c -> p (a c)").bitcast(I32).rearrange("p (b t m x) -> p b t m x", b=4, t=PACK, x=2),
             in_=w2_raw[:].rearrange("p a c -> p (a c)").bitcast(I32).rearrange("p (b m t x) -> p b t m x", b=4, t=PACK, x=2),
+        )
+
+        w2_s = sb("w2_s", [P, 2, H], U8)
+        nc.vector.tensor_copy(
+            out=w2_s[:].rearrange("p a c -> p (a c)").bitcast(I32).rearrange("p (b t m) -> p b t m", b=4, t=PACK),
+            in_=w2_s_raw[:].rearrange("p a c -> p (a c)").bitcast(I32).rearrange("p (b m t) -> p b t m", b=4, t=PACK),
         )
 
         gain_turned = psum.tile([P, BANK], F32, name="gain_turned", tag="bank3")
@@ -219,7 +225,7 @@ def tile_list_syndrome_ring_decoder_kernel(
                 nc.tensor.matmul_mx(
                     out=acc[:],
                     lhsT=w2_w[:, a, 2 * c0 : 2 * (c0 + P)].bitcast(FP4X4),
-                    lhsT_scale=w2_s[a][:, c0 : c0 + P],
+                    lhsT_scale=w2_s[:, a, c0 : c0 + P],
                     rhs=v_w[a][:].bitcast(FP8X4),
                     rhs_scale=v_s[a][:],
                     start=(a == 0),
@@ -253,7 +259,7 @@ def tile_list_syndrome_ring_decoder_kernel(
                     nc.tensor.matmul_mx(
                         out=acc[:, 0:HALF],
                         lhsT=w4_w[:, a, cols].bitcast(FP8X4),
-                        lhsT_scale=w4_s[4 * a : P, cols],
+                        lhsT_scale=w4_s[:, a, cols],
                         rhs=v_w[a][:, h * HALF : (h + 1) * HALF].bitcast(FP8X4),
                         rhs_scale=v_s[a][:, h * HALF : (h + 1) * HALF],
                         start=(a == 0),

@@ -16,6 +16,7 @@ FP8X4 = mybir.dt.float8_e4m3fn_x4
 FP4X4 = mybir.dt.float4_e2m1fn_x4
 ACT = mybir.ActivationFunctionType
 MULT = mybir.AluOpType.mult
+ADD = mybir.AluOpType.add
 
 P = 128
 PACK = 4
@@ -47,7 +48,8 @@ def tile_list_syndrome_ring_decoder_kernel(
         w4_s = sb("w4_s", [P, 2, N], U8)
         v_s = [sb(f"v_s{a}", [P, S], U8) for a in range(2)]
         gain_rows = sb("gain_rows", [P, P], F32)
-        for plane in (tab_s, w2_s_raw, w4_s, v_s[1]):
+        nc.gpsimd.memset(tab_s[:].bitcast(I32), 0)
+        for plane in (v_s[1], w2_s_raw, w4_s):
             nc.vector.memset(plane[:].bitcast(I32), 0)
         nc.vector.memset(gain_rows[:], 0.0)
         ident = sb("ident", [P, P], F32)
@@ -88,19 +90,21 @@ def tile_list_syndrome_ring_decoder_kernel(
         def load_tab(a):
             nc.sync.dma_start(out=tab_w[a][:], in_=tab_words[a].rearrange("p c i -> p (c i)").bitcast(I32))
 
-        nc.sync.dma_start(idx_put[:], offs2)
-        load_page(0)
-        load_w1(0)
-        load_page(1)
-        load_w1(1)
-        load_page(2)
-        load_w3(0)
-        load_page(3)
         nc.sync.dma_start(idx_tab[:], offs)
         for q in range(4):
             nc.sync.dma_start(
                 out=tab_s[32 * q : 32 * q + 8, :].bitcast(I32), in_=tab_scales[:, 4 * q : 4 * q + 4, :].bitcast(I32)
             )
+        nc.sync.dma_start(idx_put[:], offs2)
+        load_page(0)
+        nc.vector.tensor_copy(v_s[0][:], tab_s[:].indirect(idx_tab[:]))
+        nc.sync.dma_start(out=v_s[1][0:112, :].bitcast(I32), in_=v_s[0][4:116, :].bitcast(I32))
+        load_w1(0)
+        load_page(1)
+        load_w1(1)
+        load_page(2)
+        load_page(3)
+        load_w3(0)
         load_tab(0)
         load_w3(1)
         load_scale_rows(w2_s_raw, w2_scales)
@@ -138,29 +142,38 @@ def tile_list_syndrome_ring_decoder_kernel(
                 out=w1_bf[:].rearrange("p (t m e j) -> p t m j e", t=PACK, e=4, j=PACK),
                 in_=w1_raw[g][:].rearrange("p j (m t e) -> p t m j e", t=PACK, e=4),
             )
-            w1_q.append(quantize(f"w1_{g}", w1_bf[:], BANK))
+            return w1_bf
 
         def cast_w3(g):
-            nc.scalar.copy(
-                out=w3_bf[g][:].rearrange("p (c i) t -> p c t i", i=4),
-                in_=w3_raw[g][:].rearrange("p t (c i) -> p c t i", i=4),
-            )
+            if g == 0:
+                for c0 in range(0, N, P):
+                    nc.gpsimd.tensor_scalar(
+                        w3_bf[g][:, c0 : c0 + P, :],
+                        w3_raw[g][:, :, c0 : c0 + P].rearrange("p t c -> p c t"),
+                        1.0,
+                        0.0,
+                        MULT,
+                        ADD,
+                    )
+            else:
+                nc.scalar.copy(
+                    out=w3_bf[g][:].rearrange("p (c i) t -> p c t i", i=4),
+                    in_=w3_raw[g][:].rearrange("p t (c i) -> p c t i", i=4),
+                )
 
         put_rounds(0)
-        prep_w1(0)
+        w1_q.append(quantize("w1_0", prep_w1(0)[:], BANK))
         round_page(0)
         put_rounds(1)
-        prep_w1(1)
+        w1_bf1 = prep_w1(1)
         round_page(1)
         put_rounds(2)
         cast_w3(0)
         round_page(2)
         put_rounds(3)
+        w1_q.append(quantize("w1_1", w1_bf1[:], BANK, "fresh3"))
         round_page(3)
         cast_w3(1)
-
-        nc.vector.tensor_copy(v_s[0][:], tab_s[:].indirect(idx_tab[:]))
-        nc.sync.dma_start(out=v_s[1][0:112, :].bitcast(I32), in_=v_s[0][4:116, :].bitcast(I32))
 
         page_q = []
         for h in range(2):
@@ -215,8 +228,9 @@ def tile_list_syndrome_ring_decoder_kernel(
                 nc.scalar.copy(out=window[:, h * BANK : (h + 1) * BANK], in_=acc[:])
             nc.vector.tensor_copy(picked[g][:, t, :], window[:].indirect(idx_round[:]))
 
-        def tanh_picked(g, t):
-            nc.scalar.activation(out=picked[g][:, t, :], in_=picked[g][:, t, :], func=ACT.Tanh)
+        def tanh_picked(g, h):
+            part = picked[g][:, :, h * HALF : (h + 1) * HALF]
+            nc.scalar.activation(out=part, in_=part, func=ACT.Tanh)
 
         def project_history(g, t):
             acc = psum.tile([P, BANK], F32, name=f"hist_acc{g}{t}", tag=f"bank{t}")
@@ -232,12 +246,14 @@ def tile_list_syndrome_ring_decoder_kernel(
                     stop=(a == 1),
                 )
             nc.scalar.activation(out=hist[g][:, t, :], in_=acc[:], func=ACT.Tanh)
-            nc.vector.tensor_scalar(
-                hist[g][:, t, :], hist[g][:, t, :], gains[:, PACK * g + t : PACK * g + t + 1], None, MULT
-            )
+            row_gain = gains[:, PACK * g + t : PACK * g + t + 1]
+            if g == 0:
+                nc.gpsimd.tensor_scalar(hist[g][:, t, :], hist[g][:, t, :], row_gain, 0.0, MULT, ADD)
+            else:
+                nc.vector.tensor_scalar(hist[g][:, t, :], hist[g][:, t, :], row_gain, None, MULT)
 
         def messages(g, c0, c1):
-            z_bf = sb(f"z_bf{g}_{c0}", [P, c1 - c0, PACK], BF16)
+            z_bf = sb(f"z_bf{g}_{c0}", [P, c1 - c0, PACK], BF16, f"z_bf{g}")
             nc.vector.tensor_tensor(
                 z_bf[:].rearrange("p (c i) t -> p c t i", i=4),
                 picked[g][:, :, c0:c1].rearrange("p t (c i) -> p c t i", i=4),
@@ -280,22 +296,22 @@ def tile_list_syndrome_ring_decoder_kernel(
                     stop=(g == 1),
                 )
 
-        for g in range(2):
-            for t in range(PACK):
-                project_page(g, t)
+        for t in range(PACK):
+            project_page(0, t)
         for t in range(PACK):
             project_history(0, t)
         for t in range(PACK):
-            tanh_picked(0, t)
+            project_page(1, t)
         outs = [open_out(0)]
+        for h in range(2):
+            tanh_picked(0, h)
         for t in range(PACK):
             project_history(1, t)
-        z0 = messages(0, 0, S)
         outs.append(open_out(1))
         for h in range(2):
-            mix(outs[h], 0, z0, h * HALF)
-        for t in range(PACK):
-            tanh_picked(1, t)
+            mix(outs[h], 0, messages(0, h * HALF, (h + 1) * HALF), 0)
+        for h in range(2):
+            tanh_picked(1, h)
         out_rows = out.rearrange("(n p) c -> p n c", p=P)
         for h in range(2):
             mix(outs[h], 1, messages(1, h * HALF, (h + 1) * HALF), 0)

@@ -179,8 +179,8 @@ def tile_list_syndrome_ring_decoder_kernel(
         for h in range(2):
             page_bf = sb(f"page_bf{h}", [P, BANK * PACK], BF16)
             nc.vector.tensor_copy(
-                out=page_bf[:].bitcast(F32).rearrange("p (c i u) -> p c u i", i=4, u=2),
-                in_=pairs[h][:].rearrange("p u c x -> p u (c x)").bitcast(F32).rearrange("p u (c i) -> p c u i", i=4),
+                out=page_bf[:].bitcast(F32).rearrange("p (c i u) -> p c u i", i=2, u=2),
+                in_=pairs[h][:].rearrange("p u c x -> p u (c x)").bitcast(F32).rearrange("p u (c i) -> p c u i", i=2),
             )
             page_q.append(quantize(f"page_{h}", page_bf[:], BANK))
 
@@ -253,11 +253,11 @@ def tile_list_syndrome_ring_decoder_kernel(
                 nc.vector.tensor_scalar(hist[g][:, t, :], hist[g][:, t, :], row_gain, None, MULT)
 
         def messages(g, c0, c1):
-            z_bf = sb(f"z_bf{g}_{c0}", [P, c1 - c0, PACK], BF16, f"z_bf{g}")
+            z_bf = sb(f"z_bf{g}_{c0}", [P, c1 - c0, PACK], BF16)
             nc.vector.tensor_tensor(
-                z_bf[:].rearrange("p (c i) t -> p c t i", i=4),
-                picked[g][:, :, c0:c1].rearrange("p t (c i) -> p c t i", i=4),
-                hist[g][:, :, c0:c1].rearrange("p t (c i) -> p c t i", i=4),
+                z_bf[:].rearrange("p (c i) t -> p c t i", i=2),
+                picked[g][:, :, c0:c1].rearrange("p t (c i) -> p c t i", i=2),
+                hist[g][:, :, c0:c1].rearrange("p t (c i) -> p c t i", i=2),
                 MULT,
             )
             return quantize(f"z_{g}_{c0}", z_bf[:].rearrange("p c t -> p (c t)"), c1 - c0)
@@ -318,7 +318,7 @@ def tile_list_syndrome_ring_decoder_kernel(
             for u in range(2):
                 res = sb(f"res{h}{u}", [P, 2, HALF], F32)
                 for i in range(2):
-                    if h == 1 and u == 1:
+                    if u == 1:
                         nc.vector.tensor_copy(out=res[:, i, :], in_=outs[h][2 * u + i][:, 0:HALF])
                     else:
                         nc.scalar.copy(out=res[:, i, :], in_=outs[h][2 * u + i][:, 0:HALF])

@@ -46,12 +46,15 @@ def tile_list_syndrome_ring_decoder_kernel(
         tab_s = sb("tab_s", [P, T], U8)
         w2_s_raw = sb("w2_s_raw", [P, 2, H], U8)
         w4_s = sb("w4_s", [P, 2, N], U8)
-        v_s = [sb(f"v_s{a}", [P, S], U8) for a in range(2)]
+        v_s_rows = sb("v_s_rows", [P, S], U8)
+        v_s_planes = sb("v_s_planes", [P, 2 * S], U8)
+        v_s = [v_s_planes[:, a * S : (a + 1) * S] for a in range(2)]
         gain_rows = sb("gain_rows", [P, P], F32)
-        nc.gpsimd.memset(tab_s[:].bitcast(I32), 0)
-        for plane in (v_s[1], w2_s_raw, w4_s):
-            nc.vector.memset(plane[:].bitcast(I32), 0)
-        nc.vector.memset(gain_rows[:], 0.0)
+        nc.vector.memset(tab_s[32:64, :].bitcast(I32), 0)
+        nc.vector.memset(tab_s[64:P, :].bitcast(I32), 0)
+        for plane in (v_s_planes, w2_s_raw, w4_s):
+            nc.gpsimd.memset(plane[:].bitcast(I32), 0)
+        nc.gpsimd.memset(gain_rows[:], 0.0)
         ident = sb("ident", [P, P], F32)
         make_identity(nc, ident[:])
 
@@ -64,7 +67,7 @@ def tile_list_syndrome_ring_decoder_kernel(
 
         page = [sb(f"page{t}", [P, T2], F32) for t in range(PACK)]
         fresh = [sb(f"fresh{t}", [P, S], F32) for t in range(PACK)]
-        w1_raw = [placed("w1_raw0", [P, PACK, BANK], F32, 0), sb("w1_raw1", [P, PACK, BANK], F32)]
+        w1_raw = [sb("w1_raw0", [P, PACK, BANK], F32), sb("w1_raw1", [P, PACK, BANK], F32)]
         w3_raw = [sb("w3_raw0", [P, PACK, N], F32), placed("w3_raw1", [P, PACK, N], F32, 8192)]
         tab_w = [sb(f"tab_w{a}", [P, T], I32) for a in range(2)]
         w2_raw = sb("w2_raw", [P, 2, 2 * H], U8)
@@ -91,18 +94,18 @@ def tile_list_syndrome_ring_decoder_kernel(
             nc.sync.dma_start(out=tab_w[a][:], in_=tab_words[a].rearrange("p c i -> p (c i)").bitcast(I32))
 
         nc.sync.dma_start(idx_tab[:], offs)
-        for q in range(4):
-            nc.sync.dma_start(
-                out=tab_s[32 * q : 32 * q + 8, :].bitcast(I32), in_=tab_scales[:, 4 * q : 4 * q + 4, :].bitcast(I32)
-            )
+        nc.sync.dma_start(out=tab_s[0:32, :].bitcast(I32), in_=tab_scales.rearrange("a r c -> r a c").bitcast(I32))
         nc.sync.dma_start(idx_put[:], offs2)
         load_page(0)
-        nc.vector.tensor_copy(v_s[0][:], tab_s[:].indirect(idx_tab[:]))
-        nc.sync.dma_start(out=v_s[1][0:112, :].bitcast(I32), in_=v_s[0][4:116, :].bitcast(I32))
-        load_w1(0)
+        nc.vector.tensor_copy(v_s_rows[:], tab_s[:].indirect(idx_tab[:]))
         load_page(1)
-        load_w1(1)
+        load_w1(0)
         load_page(2)
+        load_w1(1)
+        for q in range(4):
+            nc.sync.dma_start(
+                out=v_s_planes[32 * q : 32 * q + 4, :].bitcast(I32), in_=v_s_rows[8 * q : 8 * q + 8, :].bitcast(I32)
+            )
         load_page(3)
         load_w3(0)
         load_tab(0)
@@ -162,16 +165,26 @@ def tile_list_syndrome_ring_decoder_kernel(
                 )
 
         put_rounds(0)
-        w1_q.append(quantize("w1_0", prep_w1(0)[:], BANK))
         round_page(0)
+        w1_bf0 = prep_w1(0)
         put_rounds(1)
-        w1_bf1 = prep_w1(1)
+        w1_bf1 = sb("w1_bf1", [P, BANK * PACK], BF16)
+        for t in range(PACK):
+            nc.gpsimd.tensor_scalar(
+                w1_bf1[:].rearrange("p (t m e j) -> p t m e j", t=PACK, e=4, j=PACK)[:, t],
+                w1_raw[1][:].rearrange("p j (m t e) -> p t m e j", t=PACK, e=4)[:, t],
+                1.0,
+                0.0,
+                MULT,
+                ADD,
+            )
         round_page(1)
         put_rounds(2)
         cast_w3(0)
         round_page(2)
         put_rounds(3)
-        w1_q.append(quantize("w1_1", w1_bf1[:], BANK, "fresh3"))
+        w1_q.append(quantize("w1_0", w1_bf0[:], BANK, "fresh3"))
+        w1_q.append(quantize("w1_1", w1_bf1[:], BANK, "w1_bf0"))
         round_page(3)
         cast_w3(1)
 
@@ -241,7 +254,7 @@ def tile_list_syndrome_ring_decoder_kernel(
                     lhsT=w2_w[:, a, 2 * c0 : 2 * (c0 + P)].bitcast(FP4X4),
                     lhsT_scale=w2_s[:, a, c0 : c0 + P],
                     rhs=v_w[a][:].bitcast(FP8X4),
-                    rhs_scale=v_s[a][:],
+                    rhs_scale=v_s[a],
                     start=(a == 0),
                     stop=(a == 1),
                 )
@@ -262,39 +275,35 @@ def tile_list_syndrome_ring_decoder_kernel(
             )
             return quantize(f"z_{g}_{c0}", z_bf[:].rearrange("p c t -> p (c t)"), c1 - c0)
 
-        def open_out(h):
-            accs = []
-            for n in range(4):
-                if h == 0:
-                    acc = psum.tile([P, BANK], F32, name=f"out_acc{h}{n}", tag="acc", bufs=4)
-                else:
-                    acc = psum.tile([P, BANK], F32, name=f"out_acc{h}{n}", tag=f"bank{n}")
-                accs.append(acc)
+        def open_bank(c0, c1, n0, n1, tag, bufs):
+            acc = psum.tile([P, n1 - n0, c1 - c0], F32, name=f"out_acc{c0}_{n0}", tag=tag, bufs=bufs)
+            for n in range(n0, n1):
                 cols = slice(n * P, (n + 1) * P)
                 for a in range(2):
                     nc.tensor.matmul_mx(
-                        out=acc[:, 0:HALF],
+                        out=acc[:, n - n0, :],
                         lhsT=w4_w[:, a, cols].bitcast(FP8X4),
                         lhsT_scale=w4_s[:, a, cols],
-                        rhs=v_w[a][:, h * HALF : (h + 1) * HALF].bitcast(FP8X4),
-                        rhs_scale=v_s[a][:, h * HALF : (h + 1) * HALF],
-                        start=(a == 0),
+                        rhs=v_w[a][:, c0:c1].bitcast(FP8X4),
+                        rhs_scale=v_s[a][:, c0:c1],
+                        start=(n == n0 and a == 0),
                         stop=False,
                     )
-            return accs
+            return acc, c0, c1, n0, n1
 
-        def mix(accs, g, z, c0):
-            for n in range(4):
-                cols = slice(n * P, (n + 1) * P)
-                nc.tensor.matmul_mx(
-                    out=accs[n][:, 0:HALF],
-                    lhsT=w3_q[g][0][:, cols].bitcast(FP8X4),
-                    lhsT_scale=w3_q[g][1][:, cols],
-                    rhs=z[0][:, c0 : c0 + HALF].bitcast(FP8X4),
-                    rhs_scale=z[1][:, c0 : c0 + HALF],
-                    start=False,
-                    stop=(g == 1),
-                )
+        def mix(banks, g, z, z0):
+            for acc, c0, c1, n0, n1 in banks:
+                for n in range(n0, n1):
+                    cols = slice(n * P, (n + 1) * P)
+                    nc.tensor.matmul_mx(
+                        out=acc[:, n - n0, :],
+                        lhsT=w3_q[g][0][:, cols].bitcast(FP8X4),
+                        lhsT_scale=w3_q[g][1][:, cols],
+                        rhs=z[0][:, c0 - z0 : c1 - z0].bitcast(FP8X4),
+                        rhs_scale=z[1][:, c0 - z0 : c1 - z0],
+                        start=False,
+                        stop=(g == 1 and n == n1 - 1),
+                    )
 
         for t in range(PACK):
             project_page(0, t)
@@ -302,24 +311,25 @@ def tile_list_syndrome_ring_decoder_kernel(
             project_history(0, t)
         for t in range(PACK):
             project_page(1, t)
-        outs = [open_out(0)]
+        pieces = [[open_bank(0, HALF, n0, n0 + 2, "acc", 4) for n0 in (0, 2)]]
         for h in range(2):
             tanh_picked(0, h)
         for t in range(PACK):
             project_history(1, t)
-        outs.append(open_out(1))
-        for h in range(2):
-            mix(outs[h], 0, messages(0, h * HALF, (h + 1) * HALF), 0)
+        pieces.append([open_bank(HALF, HALF + P, 0, 4, "bank0", 1)])
+        pieces.append([open_bank(HALF + P, S, n0, n0 + 2, f"bank{1 + n0 // 2}", 1) for n0 in (0, 2)])
+        mix(pieces[0], 0, messages(0, 0, HALF), 0)
+        mix(pieces[1] + pieces[2], 0, messages(0, HALF, S), HALF)
         for h in range(2):
             tanh_picked(1, h)
         out_rows = out.rearrange("(n p) c -> p n c", p=P)
-        for h in range(2):
-            mix(outs[h], 1, messages(1, h * HALF, (h + 1) * HALF), 0)
-            for u in range(2):
-                res = sb(f"res{h}{u}", [P, 2, HALF], F32)
-                for i in range(2):
-                    if u == 1:
-                        nc.vector.tensor_copy(out=res[:, i, :], in_=outs[h][2 * u + i][:, 0:HALF])
-                    else:
-                        nc.scalar.copy(out=res[:, i, :], in_=outs[h][2 * u + i][:, 0:HALF])
-                nc.sync.dma_start(out=out_rows[:, 2 * u : 2 * u + 2, h * HALF : (h + 1) * HALF], in_=res[:])
+        for banks in pieces:
+            c0, c1 = banks[0][1], banks[0][2]
+            mix(banks, 1, messages(1, c0, c1), c0)
+            for acc, c0, c1, n0, n1 in banks:
+                res = sb(f"res{c0}_{n0}", [P, n1 - n0, c1 - c0], F32)
+                if c1 == S and n1 == 4:
+                    nc.vector.tensor_copy(out=res[:], in_=acc[:])
+                else:
+                    nc.scalar.copy(out=res[:], in_=acc[:])
+                nc.sync.dma_start(out=out_rows[:, n0:n1, c0:c1], in_=res[:])

@@ -44,7 +44,8 @@ def tile_list_syndrome_ring_decoder_kernel(
         idx_round = keep.tile([P, S // 16], U16, name="idx_round")
 
         tab_s = sb("tab_s", [P, T], U8)
-        w2_s_raw = sb("w2_s_raw", [P, 2, H], U8)
+        w2_s_raw = sb("w2_s_raw", [P, H], U8)
+        w2_s = sb("w2_s", [P, 2 * H], U8)
         w4_s = sb("w4_s", [P, 2, N], U8)
         v_s_rows = sb("v_s_rows", [P, S], U8)
         v_s_planes = sb("v_s_planes", [P, 2 * S], U8)
@@ -52,7 +53,7 @@ def tile_list_syndrome_ring_decoder_kernel(
         gain_rows = sb("gain_rows", [P, P], F32)
         nc.vector.memset(tab_s[32:64, :].bitcast(I32), 0)
         nc.vector.memset(tab_s[64:P, :].bitcast(I32), 0)
-        for plane in (v_s_planes, w2_s_raw, w4_s):
+        for plane in (v_s_planes, w2_s, w4_s):
             nc.gpsimd.memset(plane[:].bitcast(I32), 0)
         nc.gpsimd.memset(gain_rows[:], 0.0)
         ident = sb("ident", [P, P], F32)
@@ -63,6 +64,12 @@ def tile_list_syndrome_ring_decoder_kernel(
                 nc.sync.dma_start(
                     out=planes[r:P:32, :, :].bitcast(I32),
                     in_=rows.rearrange("a (q r) c -> r q a c", r=4)[r].bitcast(I32),
+                )
+
+        def place_scale_rows(planes, rows):
+            for q in range(4):
+                nc.sync.dma_start(
+                    out=planes[32 * q : 32 * q + 4, :].bitcast(I32), in_=rows[8 * q : 8 * q + 8, :].bitcast(I32)
                 )
 
         page = [sb(f"page{t}", [P, T2], F32) for t in range(PACK)]
@@ -101,26 +108,21 @@ def tile_list_syndrome_ring_decoder_kernel(
         load_page(1)
         load_w1(0)
         load_page(2)
-        load_w1(1)
-        for q in range(4):
-            nc.sync.dma_start(
-                out=v_s_planes[32 * q : 32 * q + 4, :].bitcast(I32), in_=v_s_rows[8 * q : 8 * q + 8, :].bitcast(I32)
-            )
-        load_page(3)
-        load_w3(0)
-        load_tab(0)
-        load_w3(1)
-        load_scale_rows(w2_s_raw, w2_scales)
-        load_tab(1)
-        nc.sync.dma_start(out=w2_raw[:].bitcast(I32), in_=w2_words.rearrange("a p c -> p a c").bitcast(I32))
-        nc.sync.dma_start(idx_round[:], offs3)
         for g in range(2):
             nc.sync.dma_start(
                 out=gain_rows[PACK * g : PACK * (g + 1), :].rearrange("t (m e) -> t m e", e=4),
                 in_=gain.rearrange("(g m t e) -> g t m e", g=2, t=PACK, e=4)[g],
             )
-        nc.sync.dma_start(out=w4_w[:], in_=w4_words.rearrange("a p c i -> p a (c i)").bitcast(I32))
-        load_scale_rows(w4_s, w4_scales)
+        nc.sync.dma_start(out=w2_s_raw[0:32, :].bitcast(I32), in_=w2_scales.rearrange("a r c -> r a c").bitcast(I32))
+        load_w1(1)
+        load_page(3)
+        load_w3(0)
+        load_tab(0)
+        place_scale_rows(v_s_planes, v_s_rows)
+        load_w3(1)
+        load_tab(1)
+        nc.sync.dma_start(out=w2_raw[:].bitcast(I32), in_=w2_words.rearrange("a p c -> p a c").bitcast(I32))
+        nc.sync.dma_start(idx_round[:], offs3)
 
         def quantize(name, grouped, width, tag=None):
             codes = sb(f"{name}_codes", [P, width], U32, tag)
@@ -149,7 +151,7 @@ def tile_list_syndrome_ring_decoder_kernel(
 
         def cast_w3(g):
             if g == 0:
-                for c0 in range(0, N, P):
+                for c0 in range(0, N // 2, P):
                     nc.gpsimd.tensor_scalar(
                         w3_bf[g][:, c0 : c0 + P, :],
                         w3_raw[g][:, :, c0 : c0 + P].rearrange("p t c -> p c t"),
@@ -197,6 +199,20 @@ def tile_list_syndrome_ring_decoder_kernel(
             )
             page_q.append(quantize(f"page_{h}", page_bf[:], BANK))
 
+        w2_s_rows = placed("w2_s_rows", [P, H], U8, 4096)
+        nc.vector.tensor_copy(
+            out=w2_s_rows[0:32, :].bitcast(I32).rearrange("p (b t m) -> p b t m", b=2, t=PACK),
+            in_=w2_s_raw[0:32, :].bitcast(I32).rearrange("p (b m t) -> p b t m", b=2, t=PACK),
+        )
+        place_scale_rows(w2_s, w2_s_rows)
+        nc.sync.dma_start(out=w4_w[:], in_=w4_words.rearrange("a p c i -> p a (c i)").bitcast(I32))
+        load_scale_rows(w4_s, w4_scales)
+
+        w3_rest = slice(N // 2, N)
+        nc.vector.tensor_copy(
+            out=w3_bf[0][:, w3_rest, :].rearrange("p (c i) t -> p c t i", i=4),
+            in_=w3_raw[0][:, :, w3_rest].rearrange("p t (c i) -> p c t i", i=4),
+        )
         v_w = [sb(f"v_w{a}", [P, S], I32) for a in range(2)]
         w3_q = []
         for a in range(2):
@@ -206,12 +222,6 @@ def tile_list_syndrome_ring_decoder_kernel(
         nc.vector.tensor_copy(
             out=w2_w[:].rearrange("p a c -> p (a c)").bitcast(I32).rearrange("p (b t m x) -> p b t m x", b=4, t=PACK, x=2),
             in_=w2_raw[:].rearrange("p a c -> p (a c)").bitcast(I32).rearrange("p (b m t x) -> p b t m x", b=4, t=PACK, x=2),
-        )
-
-        w2_s = sb("w2_s", [P, 2, H], U8)
-        nc.vector.tensor_copy(
-            out=w2_s[:].rearrange("p a c -> p (a c)").bitcast(I32).rearrange("p (b t m) -> p b t m", b=4, t=PACK),
-            in_=w2_s_raw[:].rearrange("p a c -> p (a c)").bitcast(I32).rearrange("p (b m t) -> p b t m", b=4, t=PACK),
         )
 
         gain_turned = psum.tile([P, BANK], F32, name="gain_turned", tag="bank3")
@@ -252,7 +262,7 @@ def tile_list_syndrome_ring_decoder_kernel(
                 nc.tensor.matmul_mx(
                     out=acc[:],
                     lhsT=w2_w[:, a, 2 * c0 : 2 * (c0 + P)].bitcast(FP4X4),
-                    lhsT_scale=w2_s[:, a, c0 : c0 + P],
+                    lhsT_scale=w2_s[:, a * H + c0 : a * H + c0 + P],
                     rhs=v_w[a][:].bitcast(FP8X4),
                     rhs_scale=v_s[a],
                     start=(a == 0),

@@ -43,8 +43,15 @@ def tile_list_syndrome_ring_decoder_kernel(
         idx_put = keep.tile([P, S // 16], U16, name="idx_put")
         idx_round = keep.tile([P, S // 16], U16, name="idx_round")
 
+        at_fresh3 = 0
+        at_ta = 2048
+        at_late = at_ta + 2048
+        at_tab0 = at_late + 8192
+        at_tab1 = at_tab0 + 8192
+
         tab_s = sb("tab_s", [P, T], U8)
         w2_s_raw = sb("w2_s_raw", [P, H], U8)
+        w2_s_rows = sb("w2_s_rows", [P, H], U8)
         w2_s = sb("w2_s", [P, 2 * H], U8)
         w4_s = sb("w4_s", [P, 2, N], U8)
         v_s_rows = sb("v_s_rows", [P, S], U8)
@@ -53,9 +60,9 @@ def tile_list_syndrome_ring_decoder_kernel(
         gain_rows = sb("gain_rows", [P, P], F32)
         nc.vector.memset(tab_s[32:64, :].bitcast(I32), 0)
         nc.vector.memset(tab_s[64:P, :].bitcast(I32), 0)
+        nc.gpsimd.memset(gain_rows[:], 0.0)
         for plane in (v_s_planes, w2_s, w4_s):
             nc.gpsimd.memset(plane[:].bitcast(I32), 0)
-        nc.gpsimd.memset(gain_rows[:], 0.0)
         ident = sb("ident", [P, P], F32)
         make_identity(nc, ident[:])
 
@@ -73,10 +80,12 @@ def tile_list_syndrome_ring_decoder_kernel(
                 )
 
         page = [sb(f"page{t}", [P, T2], F32) for t in range(PACK)]
-        fresh = [sb(f"fresh{t}", [P, S], F32) for t in range(PACK)]
-        w1_raw = [sb("w1_raw0", [P, PACK, BANK], F32), sb("w1_raw1", [P, PACK, BANK], F32)]
-        w3_raw = [sb("w3_raw0", [P, PACK, N], F32), placed("w3_raw1", [P, PACK, N], F32, 8192)]
-        tab_w = [sb(f"tab_w{a}", [P, T], I32) for a in range(2)]
+        fresh = [sb(f"fresh{t}", [P, S], F32) for t in range(PACK - 1)]
+        fresh.append(placed("fresh3", [P, S], F32, at_fresh3))
+        w1_first = sb("w1_first", [P, PACK, BANK], F32)
+        w1_second = [sb(f"w1_second{h}", [P, PACK, HALF], F32) for h in range(2)]
+        w3_raw = [sb("w3_raw0", [P, PACK, N], F32), placed("w3_raw1", [P, PACK, N], F32, at_late)]
+        tab_w = [placed("tab_w0", [P, T], I32, at_tab0), placed("tab_w1", [P, T], I32, at_tab1)]
         w2_raw = sb("w2_raw", [P, 2, 2 * H], U8)
         w4_w = sb("w4_w", [P, 2, N], I32)
         gains = sb("gains", [P, 2 * PACK], F32)
@@ -89,9 +98,6 @@ def tile_list_syndrome_ring_decoder_kernel(
         def load_page(t):
             nc.sync.dma_start(out=fresh[t][:], in_=xs_rows[:, t, :])
             nc.sync.dma_start(out=page[t][:], in_=base_rows[:, t, :])
-
-        def load_w1(g):
-            nc.sync.dma_start(out=w1_raw[g][:], in_=w1_rows[:, :, g * BANK : (g + 1) * BANK])
 
         def load_w3(g):
             for t in range(PACK):
@@ -106,32 +112,48 @@ def tile_list_syndrome_ring_decoder_kernel(
         load_page(0)
         nc.vector.tensor_copy(v_s_rows[:], tab_s[:].indirect(idx_tab[:]))
         load_page(1)
-        load_w1(0)
-        load_page(2)
+        nc.sync.dma_start(out=w1_first[:], in_=w1_rows[:, :, 0:BANK])
         for g in range(2):
             nc.sync.dma_start(
                 out=gain_rows[PACK * g : PACK * (g + 1), :].rearrange("t (m e) -> t m e", e=4),
                 in_=gain.rearrange("(g m t e) -> g t m e", g=2, t=PACK, e=4)[g],
             )
         nc.sync.dma_start(out=w2_s_raw[0:32, :].bitcast(I32), in_=w2_scales.rearrange("a r c -> r a c").bitcast(I32))
-        load_w1(1)
-        load_page(3)
-        load_w3(0)
-        load_tab(0)
-        place_scale_rows(v_s_planes, v_s_rows)
-        load_w3(1)
-        load_tab(1)
-        nc.sync.dma_start(out=w2_raw[:].bitcast(I32), in_=w2_words.rearrange("a p c -> p a c").bitcast(I32))
         nc.sync.dma_start(idx_round[:], offs3)
+        load_page(2)
+        load_w3(0)
+        load_page(3)
+        for h in range(2):
+            nc.sync.dma_start(out=w1_second[h][:], in_=w1_rows[:, :, BANK + h * HALF : BANK + (h + 1) * HALF])
+        load_w3(1)
+        load_tab(0)
+        nc.sync.dma_start(out=w2_raw[:].bitcast(I32), in_=w2_words.rearrange("a p c -> p a c").bitcast(I32))
+        load_tab(1)
 
-        def quantize(name, grouped, width, tag=None):
-            codes = sb(f"{name}_codes", [P, width], U32, tag)
-            scales = sb(f"{name}_scales", [P, width], U8)
+        nc.gpsimd.tensor_copy(
+            out=w2_s_rows[0:32, :].bitcast(I32).rearrange("p (b t m) -> p b t m", b=2, t=PACK),
+            in_=w2_s_raw[0:32, :].bitcast(I32).rearrange("p (b m t) -> p b t m", b=2, t=PACK),
+        )
+        place_scale_rows(v_s_planes, v_s_rows)
+        place_scale_rows(w2_s, w2_s_rows)
+        nc.sync.dma_start(out=w4_w[:], in_=w4_words.rearrange("a p c i -> p a (c i)").bitcast(I32))
+        load_scale_rows(w4_s, w4_scales)
+
+        gain_turned = psum.tile([P, BANK], F32, name="gain_turned", tag="bank3")
+        nc.tensor.transpose(gain_turned[:, 0:P], gain_rows[:], ident[:])
+        nc.scalar.copy(out=gains[:], in_=gain_turned[:, 0 : 2 * PACK])
+
+        def quantize(name, grouped, width, scales_at=None):
+            codes = sb(f"{name}_codes", [P, width], U32)
+            if scales_at is None:
+                scales = sb(f"{name}_scales", [P, width], U8)
+            else:
+                scales = placed(f"{name}_scales", [P, width], U8, scales_at)
             nc.vector.quantize_mx(out=codes[:].bitcast(FP8X4), scales=scales[:], in_=grouped)
             return codes, scales
 
-        pairs = [placed(f"pairs{h}", [P, 2, BANK, 2], BF16, 4096 * h) for h in range(2)]
-        w1_q = []
+        pairs = [sb(f"pairs{h}", [P, 2, BANK, 2], BF16) for h in range(2)]
+        w1_bf = [sb(f"w1_bf{g}", [P, BANK * PACK], BF16) for g in range(2)]
         w3_bf = [sb(f"w3_bf{g}", [P, N, PACK], BF16) for g in range(2)]
 
         def put_rounds(t):
@@ -141,99 +163,59 @@ def tile_list_syndrome_ring_decoder_kernel(
             for h in range(2):
                 nc.scalar.copy(out=pairs[h][:, t // 2, :, t % 2], in_=page[t][:, h * BANK : (h + 1) * BANK])
 
-        def prep_w1(g):
-            w1_bf = sb(f"w1_bf{g}", [P, BANK * PACK], BF16)
-            nc.scalar.copy(
-                out=w1_bf[:].rearrange("p (t m e j) -> p t m j e", t=PACK, e=4, j=PACK),
-                in_=w1_raw[g][:].rearrange("p j (m t e) -> p t m j e", t=PACK, e=4),
-            )
-            return w1_bf
-
-        def cast_w3(g):
-            if g == 0:
-                for c0 in range(0, N // 2, P):
-                    nc.gpsimd.tensor_scalar(
-                        w3_bf[g][:, c0 : c0 + P, :],
-                        w3_raw[g][:, :, c0 : c0 + P].rearrange("p t c -> p c t"),
-                        1.0,
-                        0.0,
-                        MULT,
-                        ADD,
-                    )
-            else:
-                nc.scalar.copy(
-                    out=w3_bf[g][:].rearrange("p (c i) t -> p c t i", i=4),
-                    in_=w3_raw[g][:].rearrange("p t (c i) -> p c t i", i=4),
-                )
-
         put_rounds(0)
         round_page(0)
-        w1_bf0 = prep_w1(0)
         put_rounds(1)
-        w1_bf1 = sb("w1_bf1", [P, BANK * PACK], BF16)
-        for t in range(PACK):
-            nc.gpsimd.tensor_scalar(
-                w1_bf1[:].rearrange("p (t m e j) -> p t m e j", t=PACK, e=4, j=PACK)[:, t],
-                w1_raw[1][:].rearrange("p j (m t e) -> p t m e j", t=PACK, e=4)[:, t],
-                1.0,
-                0.0,
-                MULT,
-                ADD,
-            )
         round_page(1)
+        nc.scalar.copy(
+            out=w1_bf[0][:].rearrange("p (t m e j) -> p t m j e", t=PACK, e=4, j=PACK),
+            in_=w1_first[:].rearrange("p j (m t e) -> p t m j e", t=PACK, e=4),
+        )
         put_rounds(2)
-        cast_w3(0)
         round_page(2)
+        for c0 in range(0, N, P):
+            nc.gpsimd.tensor_scalar(
+                w3_bf[0][:, c0 : c0 + P, :], w3_raw[0][:, :, c0 : c0 + P].rearrange("p t c -> p c t"), 1.0, 0.0, MULT, ADD
+            )
         put_rounds(3)
-        w1_q.append(quantize("w1_0", w1_bf0[:], BANK, "fresh3"))
-        w1_q.append(quantize("w1_1", w1_bf1[:], BANK, "w1_bf0"))
         round_page(3)
-        cast_w3(1)
-
-        page_q = []
         for h in range(2):
-            page_bf = sb(f"page_bf{h}", [P, BANK * PACK], BF16)
+            for m0 in (0, 8):
+                nc.gpsimd.tensor_scalar(
+                    w1_bf[1][:].rearrange("p (t m e j) -> p m t e j", t=PACK, e=4, j=PACK)[:, 16 * h + m0 : 16 * h + m0 + 8],
+                    w1_second[h][:].rearrange("p j (m t e) -> p m t e j", t=PACK, e=4)[:, m0 : m0 + 8],
+                    1.0,
+                    0.0,
+                    MULT,
+                    ADD,
+                )
+        nc.scalar.copy(
+            out=w3_bf[1][:].rearrange("p (c i) t -> p c t i", i=4),
+            in_=w3_raw[1][:].rearrange("p t (c i) -> p c t i", i=4),
+        )
+        w1_q = [quantize("w1_0", w1_bf[0][:], BANK, at_fresh3)]
+        w3_q = [quantize("w3_0", w3_bf[0][:].rearrange("p c t -> p (c t)"), N, at_fresh3 + 512)]
+
+        page_bf = [sb(f"page_bf{h}", [P, BANK * PACK], BF16) for h in range(2)]
+        for h in range(2):
             nc.vector.tensor_copy(
-                out=page_bf[:].bitcast(F32).rearrange("p (c i u) -> p c u i", i=2, u=2),
+                out=page_bf[h][:].bitcast(F32).rearrange("p (c i u) -> p c u i", i=2, u=2),
                 in_=pairs[h][:].rearrange("p u c x -> p u (c x)").bitcast(F32).rearrange("p u (c i) -> p c u i", i=2),
             )
-            page_q.append(quantize(f"page_{h}", page_bf[:], BANK))
+        page_q = [quantize(f"page_{h}", page_bf[h][:], BANK) for h in range(2)]
+        w1_q.append(quantize("w1_1", w1_bf[1][:], BANK))
 
-        w2_s_rows = placed("w2_s_rows", [P, H], U8, 4096)
-        nc.vector.tensor_copy(
-            out=w2_s_rows[0:32, :].bitcast(I32).rearrange("p (b t m) -> p b t m", b=2, t=PACK),
-            in_=w2_s_raw[0:32, :].bitcast(I32).rearrange("p (b m t) -> p b t m", b=2, t=PACK),
-        )
-        place_scale_rows(w2_s, w2_s_rows)
-        nc.sync.dma_start(out=w4_w[:], in_=w4_words.rearrange("a p c i -> p a (c i)").bitcast(I32))
-        load_scale_rows(w4_s, w4_scales)
-
-        w3_rest = slice(N // 2, N)
-        nc.vector.tensor_copy(
-            out=w3_bf[0][:, w3_rest, :].rearrange("p (c i) t -> p c t i", i=4),
-            in_=w3_raw[0][:, :, w3_rest].rearrange("p t (c i) -> p c t i", i=4),
-        )
         v_w = [sb(f"v_w{a}", [P, S], I32) for a in range(2)]
-        w3_q = []
-        for a in range(2):
+
+        def pick_history(a):
             nc.vector.tensor_copy(v_w[a][:].bitcast(U32), tab_w[a][:].bitcast(U32).indirect(idx_tab[:]))
-            w3_q.append(quantize(f"w3_{a}", w3_bf[a][:].rearrange("p c t -> p (c t)"), N, f"page_bf{1 - a}"))
-        w2_w = sb("w2_w", [P, 2, 2 * H], U8)
-        nc.vector.tensor_copy(
-            out=w2_w[:].rearrange("p a c -> p (a c)").bitcast(I32).rearrange("p (b t m x) -> p b t m x", b=4, t=PACK, x=2),
-            in_=w2_raw[:].rearrange("p a c -> p (a c)").bitcast(I32).rearrange("p (b m t x) -> p b t m x", b=4, t=PACK, x=2),
-        )
 
-        gain_turned = psum.tile([P, BANK], F32, name="gain_turned", tag="bank3")
-        nc.tensor.transpose(gain_turned[:, 0:P], gain_rows[:], ident[:])
-        nc.scalar.copy(out=gains[:], in_=gain_turned[:, 0 : 2 * PACK])
-
-        picked = [sb(f"picked{g}", [P, PACK, S], F32) for g in range(2)]
+        picked = [placed("picked0", [P, PACK, S], F32, at_tab0), placed("picked1", [P, PACK, S], F32, at_tab1 + 512)]
         hist = [sb(f"hist{g}", [P, PACK, S], F32) for g in range(2)]
 
         def project_page(g, t):
             if g == 0 and t < 2:
-                window = placed(f"rounds{g}{t}", [P, T2], F32, 8192 + 4096 * t)
+                window = placed(f"rounds{g}{t}", [P, T2], F32, at_late + 4096 * t)
             else:
                 window = sb(f"rounds{g}{t}", [P, T2], F32)
             cols = slice(t * P, (t + 1) * P)
@@ -251,9 +233,23 @@ def tile_list_syndrome_ring_decoder_kernel(
                 nc.scalar.copy(out=window[:, h * BANK : (h + 1) * BANK], in_=acc[:])
             nc.vector.tensor_copy(picked[g][:, t, :], window[:].indirect(idx_round[:]))
 
+        w2_w = []
+
+        def deal_w2(g):
+            dealt = placed(f"w2_w{g}", [P, 2, H], U8, at_late + 2048 * g)
+            nc.gpsimd.tensor_copy(
+                out=dealt[:].bitcast(I32).rearrange("p a (t m x) -> p a t m x", t=PACK, x=2),
+                in_=w2_raw[:, :, g * H : (g + 1) * H].bitcast(I32).rearrange("p a (m t x) -> p a t m x", t=PACK, x=2),
+            )
+            w2_w.append(dealt)
+
         def tanh_picked(g, h):
-            part = picked[g][:, :, h * HALF : (h + 1) * HALF]
-            nc.scalar.activation(out=part, in_=part, func=ACT.Tanh)
+            if h == 0:
+                bent = placed(f"bent{g}0", [P, PACK, HALF], F32, at_ta)
+            else:
+                bent = sb(f"bent{g}1", [P, PACK, HALF], F32, "bent1")
+            nc.scalar.activation(out=bent[:], in_=picked[g][:, :, h * HALF : (h + 1) * HALF], func=ACT.Tanh)
+            return bent
 
         def project_history(g, t):
             acc = psum.tile([P, BANK], F32, name=f"hist_acc{g}{t}", tag=f"bank{t}")
@@ -261,7 +257,7 @@ def tile_list_syndrome_ring_decoder_kernel(
             for a in range(2):
                 nc.tensor.matmul_mx(
                     out=acc[:],
-                    lhsT=w2_w[:, a, 2 * c0 : 2 * (c0 + P)].bitcast(FP4X4),
+                    lhsT=w2_w[g][:, a, 2 * t * P : 2 * (t + 1) * P].bitcast(FP4X4),
                     lhsT_scale=w2_s[:, a * H + c0 : a * H + c0 + P],
                     rhs=v_w[a][:].bitcast(FP8X4),
                     rhs_scale=v_s[a],
@@ -269,39 +265,48 @@ def tile_list_syndrome_ring_decoder_kernel(
                     stop=(a == 1),
                 )
             nc.scalar.activation(out=hist[g][:, t, :], in_=acc[:], func=ACT.Tanh)
+
+        def apply_gain(g, t):
             row_gain = gains[:, PACK * g + t : PACK * g + t + 1]
-            if g == 0:
+            if g == 0 or t < 2:
                 nc.gpsimd.tensor_scalar(hist[g][:, t, :], hist[g][:, t, :], row_gain, 0.0, MULT, ADD)
             else:
                 nc.vector.tensor_scalar(hist[g][:, t, :], hist[g][:, t, :], row_gain, None, MULT)
 
-        def messages(g, c0, c1):
+        def product(g, bent, c0, c1):
             z_bf = sb(f"z_bf{g}_{c0}", [P, c1 - c0, PACK], BF16)
+            b0 = c0 % HALF
             nc.vector.tensor_tensor(
                 z_bf[:].rearrange("p (c i) t -> p c t i", i=2),
-                picked[g][:, :, c0:c1].rearrange("p t (c i) -> p c t i", i=2),
+                bent[:, :, b0 : b0 + c1 - c0].rearrange("p t (c i) -> p c t i", i=2),
                 hist[g][:, :, c0:c1].rearrange("p t (c i) -> p c t i", i=2),
                 MULT,
             )
+            return z_bf
+
+        def quantize_z(g, z_bf, c0, c1):
             return quantize(f"z_{g}_{c0}", z_bf[:].rearrange("p c t -> p (c t)"), c1 - c0)
 
         def open_bank(c0, c1, n0, n1, tag, bufs):
             acc = psum.tile([P, n1 - n0, c1 - c0], F32, name=f"out_acc{c0}_{n0}", tag=tag, bufs=bufs)
-            for n in range(n0, n1):
-                cols = slice(n * P, (n + 1) * P)
-                for a in range(2):
-                    nc.tensor.matmul_mx(
-                        out=acc[:, n - n0, :],
-                        lhsT=w4_w[:, a, cols].bitcast(FP8X4),
-                        lhsT_scale=w4_s[:, a, cols],
-                        rhs=v_w[a][:, c0:c1].bitcast(FP8X4),
-                        rhs_scale=v_s[a][:, c0:c1],
-                        start=(n == n0 and a == 0),
-                        stop=False,
-                    )
             return acc, c0, c1, n0, n1
 
-        def mix(banks, g, z, z0):
+        def add_prior(banks, first):
+            for acc, c0, c1, n0, n1 in banks:
+                for n in range(n0, n1):
+                    cols = slice(n * P, (n + 1) * P)
+                    for a in range(2):
+                        nc.tensor.matmul_mx(
+                            out=acc[:, n - n0, :],
+                            lhsT=w4_w[:, a, cols].bitcast(FP8X4),
+                            lhsT_scale=w4_s[:, a, cols],
+                            rhs=v_w[a][:, c0:c1].bitcast(FP8X4),
+                            rhs_scale=v_s[a][:, c0:c1],
+                            start=(first and n == n0 and a == 0),
+                            stop=False,
+                        )
+
+        def mix(banks, g, z, z0, first=False):
             for acc, c0, c1, n0, n1 in banks:
                 for n in range(n0, n1):
                     cols = slice(n * P, (n + 1) * P)
@@ -311,34 +316,46 @@ def tile_list_syndrome_ring_decoder_kernel(
                         lhsT_scale=w3_q[g][1][:, cols],
                         rhs=z[0][:, c0 - z0 : c1 - z0].bitcast(FP8X4),
                         rhs_scale=z[1][:, c0 - z0 : c1 - z0],
-                        start=False,
+                        start=(first and n == n0),
                         stop=(g == 1 and n == n1 - 1),
                     )
 
+        pick_history(0)
         for t in range(PACK):
             project_page(0, t)
-        for t in range(PACK):
-            project_history(0, t)
+        for g in range(2):
+            deal_w2(g)
+        pick_history(1)
+        w3_q.append(quantize("w3_1", w3_bf[1][:].rearrange("p c t -> p (c t)"), N, at_tab1))
         for t in range(PACK):
             project_page(1, t)
+        for g, t in [(0, 0), (0, 1), (0, 2), (0, 3), (1, 0), (1, 1)]:
+            project_history(g, t)
+            apply_gain(g, t)
         pieces = [[open_bank(0, HALF, n0, n0 + 2, "acc", 4) for n0 in (0, 2)]]
-        for h in range(2):
-            tanh_picked(0, h)
-        for t in range(PACK):
+        add_prior(pieces[0], True)
+        bent = [tanh_picked(0, h) for h in range(2)]
+        for t in (2, 3):
             project_history(1, t)
         pieces.append([open_bank(HALF, HALF + P, 0, 4, "bank0", 1)])
         pieces.append([open_bank(HALF + P, S, n0, n0 + 2, f"bank{1 + n0 // 2}", 1) for n0 in (0, 2)])
-        mix(pieces[0], 0, messages(0, 0, HALF), 0)
-        mix(pieces[1] + pieces[2], 0, messages(0, HALF, S), HALF)
-        for h in range(2):
-            tanh_picked(1, h)
+        add_prior(pieces[1], True)
+        z_first = [product(0, bent[h], h * HALF, (h + 1) * HALF) for h in range(2)]
+        mix(pieces[0], 0, quantize_z(0, z_first[0], 0, HALF), 0)
+        for t in (2, 3):
+            apply_gain(1, t)
+        z_rest = quantize_z(0, z_first[1], HALF, S)
+        mix(pieces[1], 0, z_rest, HALF)
+        mix(pieces[2], 0, z_rest, HALF, True)
+        add_prior(pieces[2], False)
+        bent = [tanh_picked(1, h) for h in range(2)]
         out_rows = out.rearrange("(n p) c -> p n c", p=P)
         for banks in pieces:
             c0, c1 = banks[0][1], banks[0][2]
-            mix(banks, 1, messages(1, c0, c1), c0)
+            mix(banks, 1, quantize_z(1, product(1, bent[c0 // HALF], c0, c1), c0, c1), c0)
             for acc, c0, c1, n0, n1 in banks:
                 res = sb(f"res{c0}_{n0}", [P, n1 - n0, c1 - c0], F32)
-                if c1 == S and n1 == 4:
+                if c0 >= HALF and n1 == 4:
                     nc.vector.tensor_copy(out=res[:], in_=acc[:])
                 else:
                     nc.scalar.copy(out=res[:], in_=acc[:])

@@ -44,10 +44,13 @@ def tile_list_syndrome_ring_decoder_kernel(
         idx_round = keep.tile([P, S // 16], U16, name="idx_round")
 
         at_fresh3 = 0
-        at_ta = 2048
-        at_late = at_ta + 2048
-        at_tab0 = at_late + 8192
-        at_tab1 = at_tab0 + 8192
+        at_last_windows = [2048, 2048 + 8192]
+        at_dealt = [at + 3072 for at in at_last_windows]
+        at_bent = [at + 4096 for at in at_last_windows]
+        at_window5 = 2048 + 2 * 8192
+        at_late = at_window5 + 4096
+        at_tab1 = at_late + 8192
+        at_w3 = at_tab1 + 8192 + 512
 
         tab_s = sb("tab_s", [P, T], U8)
         w2_s_raw = sb("w2_s_raw", [P, H], U8)
@@ -82,10 +85,9 @@ def tile_list_syndrome_ring_decoder_kernel(
         page = [sb(f"page{t}", [P, T2], F32) for t in range(PACK)]
         fresh = [sb(f"fresh{t}", [P, S], F32) for t in range(PACK - 1)]
         fresh.append(placed("fresh3", [P, S], F32, at_fresh3))
-        w1_first = sb("w1_first", [P, PACK, BANK], F32)
-        w1_second = [sb(f"w1_second{h}", [P, PACK, HALF], F32) for h in range(2)]
-        w3_raw = [sb("w3_raw0", [P, PACK, N], F32), placed("w3_raw1", [P, PACK, N], F32, at_late)]
-        tab_w = [placed("tab_w0", [P, T], I32, at_tab0), placed("tab_w1", [P, T], I32, at_tab1)]
+        w1_raw = [sb("w1_raw0", [P, PACK, BANK], F32), placed("w1_raw1", [P, PACK, BANK], F32, at_late)]
+        w3_raw = [sb("w3_raw0", [P, PACK, N], F32), placed("w3_raw1", [P, PACK, N], F32, at_w3)]
+        tab_w = [sb("tab_w0", [P, T], I32), placed("tab_w1", [P, T], I32, at_tab1)]
         w2_raw = sb("w2_raw", [P, 2, 2 * H], U8)
         w4_w = sb("w4_w", [P, 2, N], I32)
         gains = sb("gains", [P, 2 * PACK], F32)
@@ -112,7 +114,7 @@ def tile_list_syndrome_ring_decoder_kernel(
         load_page(0)
         nc.vector.tensor_copy(v_s_rows[:], tab_s[:].indirect(idx_tab[:]))
         load_page(1)
-        nc.sync.dma_start(out=w1_first[:], in_=w1_rows[:, :, 0:BANK])
+        nc.sync.dma_start(out=w1_raw[0][:], in_=w1_rows[:, :, 0:BANK])
         for g in range(2):
             nc.sync.dma_start(
                 out=gain_rows[PACK * g : PACK * (g + 1), :].rearrange("t (m e) -> t m e", e=4),
@@ -123,12 +125,9 @@ def tile_list_syndrome_ring_decoder_kernel(
         load_page(2)
         load_w3(0)
         load_page(3)
-        for h in range(2):
-            nc.sync.dma_start(out=w1_second[h][:], in_=w1_rows[:, :, BANK + h * HALF : BANK + (h + 1) * HALF])
-        load_w3(1)
-        load_tab(0)
         nc.sync.dma_start(out=w2_raw[:].bitcast(I32), in_=w2_words.rearrange("a p c -> p a c").bitcast(I32))
-        load_tab(1)
+        nc.sync.dma_start(out=w1_raw[1][:], in_=w1_rows[:, :, BANK : 2 * BANK])
+        load_tab(0)
 
         nc.gpsimd.tensor_copy(
             out=w2_s_rows[0:32, :].bitcast(I32).rearrange("p (b t m) -> p b t m", b=2, t=PACK),
@@ -136,6 +135,8 @@ def tile_list_syndrome_ring_decoder_kernel(
         )
         place_scale_rows(v_s_planes, v_s_rows)
         place_scale_rows(w2_s, w2_s_rows)
+        load_tab(1)
+        load_w3(1)
         nc.sync.dma_start(out=w4_w[:], in_=w4_words.rearrange("a p c i -> p a (c i)").bitcast(I32))
         load_scale_rows(w4_s, w4_scales)
 
@@ -154,7 +155,28 @@ def tile_list_syndrome_ring_decoder_kernel(
 
         pairs = [sb(f"pairs{h}", [P, 2, BANK, 2], BF16) for h in range(2)]
         w1_bf = [sb(f"w1_bf{g}", [P, BANK * PACK], BF16) for g in range(2)]
-        w3_bf = [sb(f"w3_bf{g}", [P, N, PACK], BF16) for g in range(2)]
+
+        def round_w1(g):
+            nc.scalar.copy(
+                out=w1_bf[g][:].rearrange("p (t m e j) -> p t m j e", t=PACK, e=4, j=PACK),
+                in_=w1_raw[g][:].rearrange("p j (m t e) -> p t m j e", t=PACK, e=4),
+            )
+
+        def round_w3(g, tag):
+            grouped = sb(f"w3_bf{g}", [P, N, PACK], BF16, tag)
+            for c0 in range(0, N, P):
+                nc.gpsimd.tensor_scalar(
+                    grouped[:, c0 : c0 + P, :], w3_raw[g][:, :, c0 : c0 + P].rearrange("p t c -> p c t"), 1.0, 0.0, MULT, ADD
+                )
+            return grouped[:].rearrange("p c t -> p (c t)")
+
+        def deal_w2(g):
+            dealt = placed(f"w2_w{g}", [P, 2, H], U8, at_dealt[g])
+            nc.gpsimd.tensor_copy(
+                out=dealt[:].bitcast(I32).rearrange("p a (t m x) -> p a t m x", t=PACK, x=2),
+                in_=w2_raw[:, :, g * H : (g + 1) * H].bitcast(I32).rearrange("p a (m t x) -> p a t m x", t=PACK, x=2),
+            )
+            return dealt
 
         def put_rounds(t):
             nc.vector.tensor_copy(page[t][:].indirect(idx_put[:]), fresh[t][:])
@@ -167,34 +189,16 @@ def tile_list_syndrome_ring_decoder_kernel(
         round_page(0)
         put_rounds(1)
         round_page(1)
-        nc.scalar.copy(
-            out=w1_bf[0][:].rearrange("p (t m e j) -> p t m j e", t=PACK, e=4, j=PACK),
-            in_=w1_first[:].rearrange("p j (m t e) -> p t m j e", t=PACK, e=4),
-        )
+        round_w1(0)
         put_rounds(2)
         round_page(2)
-        for c0 in range(0, N, P):
-            nc.gpsimd.tensor_scalar(
-                w3_bf[0][:, c0 : c0 + P, :], w3_raw[0][:, :, c0 : c0 + P].rearrange("p t c -> p c t"), 1.0, 0.0, MULT, ADD
-            )
+        w3_first = round_w3(0, None)
         put_rounds(3)
         round_page(3)
-        for h in range(2):
-            for m0 in (0, 8):
-                nc.gpsimd.tensor_scalar(
-                    w1_bf[1][:].rearrange("p (t m e j) -> p m t e j", t=PACK, e=4, j=PACK)[:, 16 * h + m0 : 16 * h + m0 + 8],
-                    w1_second[h][:].rearrange("p j (m t e) -> p m t e j", t=PACK, e=4)[:, m0 : m0 + 8],
-                    1.0,
-                    0.0,
-                    MULT,
-                    ADD,
-                )
-        nc.scalar.copy(
-            out=w3_bf[1][:].rearrange("p (c i) t -> p c t i", i=4),
-            in_=w3_raw[1][:].rearrange("p t (c i) -> p c t i", i=4),
-        )
+        w2_w = [deal_w2(g) for g in range(2)]
+        round_w1(1)
         w1_q = [quantize("w1_0", w1_bf[0][:], BANK, at_fresh3)]
-        w3_q = [quantize("w3_0", w3_bf[0][:].rearrange("p c t -> p (c t)"), N, at_fresh3 + 512)]
+        w3_q = [quantize("w3_0", w3_first, N, at_fresh3 + 512)]
 
         page_bf = [sb(f"page_bf{h}", [P, BANK * PACK], BF16) for h in range(2)]
         for h in range(2):
@@ -203,19 +207,21 @@ def tile_list_syndrome_ring_decoder_kernel(
                 in_=pairs[h][:].rearrange("p u c x -> p u (c x)").bitcast(F32).rearrange("p u (c i) -> p c u i", i=2),
             )
         page_q = [quantize(f"page_{h}", page_bf[h][:], BANK) for h in range(2)]
-        w1_q.append(quantize("w1_1", w1_bf[1][:], BANK))
 
         v_w = [sb(f"v_w{a}", [P, S], I32) for a in range(2)]
 
         def pick_history(a):
             nc.vector.tensor_copy(v_w[a][:].bitcast(U32), tab_w[a][:].bitcast(U32).indirect(idx_tab[:]))
 
-        picked = [placed("picked0", [P, PACK, S], F32, at_tab0), placed("picked1", [P, PACK, S], F32, at_tab1 + 512)]
+        picked = [placed("picked0", [P, PACK, S], F32, at_tab1 + 512), sb("picked1", [P, PACK, S], F32)]
         hist = [sb(f"hist{g}", [P, PACK, S], F32) for g in range(2)]
+        scaled = [placed("scaled0", [P, PACK, S], F32, at_w3), hist[1]]
 
         def project_page(g, t):
             if g == 0 and t < 2:
                 window = placed(f"rounds{g}{t}", [P, T2], F32, at_late + 4096 * t)
+            elif g == 1 and t > 0:
+                window = placed(f"rounds{g}{t}", [P, T2], F32, at_window5 if t == 1 else at_last_windows[t - 2])
             else:
                 window = sb(f"rounds{g}{t}", [P, T2], F32)
             cols = slice(t * P, (t + 1) * P)
@@ -233,21 +239,8 @@ def tile_list_syndrome_ring_decoder_kernel(
                 nc.scalar.copy(out=window[:, h * BANK : (h + 1) * BANK], in_=acc[:])
             nc.vector.tensor_copy(picked[g][:, t, :], window[:].indirect(idx_round[:]))
 
-        w2_w = []
-
-        def deal_w2(g):
-            dealt = placed(f"w2_w{g}", [P, 2, H], U8, at_late + 2048 * g)
-            nc.gpsimd.tensor_copy(
-                out=dealt[:].bitcast(I32).rearrange("p a (t m x) -> p a t m x", t=PACK, x=2),
-                in_=w2_raw[:, :, g * H : (g + 1) * H].bitcast(I32).rearrange("p a (m t x) -> p a t m x", t=PACK, x=2),
-            )
-            w2_w.append(dealt)
-
         def tanh_picked(g, h):
-            if h == 0:
-                bent = placed(f"bent{g}0", [P, PACK, HALF], F32, at_ta)
-            else:
-                bent = sb(f"bent{g}1", [P, PACK, HALF], F32, "bent1")
+            bent = placed(f"bent{g}{h}", [P, PACK, HALF], F32, at_bent[h])
             nc.scalar.activation(out=bent[:], in_=picked[g][:, :, h * HALF : (h + 1) * HALF], func=ACT.Tanh)
             return bent
 
@@ -268,8 +261,8 @@ def tile_list_syndrome_ring_decoder_kernel(
 
         def apply_gain(g, t):
             row_gain = gains[:, PACK * g + t : PACK * g + t + 1]
-            if g == 0 or t < 2:
-                nc.gpsimd.tensor_scalar(hist[g][:, t, :], hist[g][:, t, :], row_gain, 0.0, MULT, ADD)
+            if g == 0:
+                nc.gpsimd.tensor_scalar(scaled[g][:, t, :], hist[g][:, t, :], row_gain, 0.0, MULT, ADD)
             else:
                 nc.vector.tensor_scalar(hist[g][:, t, :], hist[g][:, t, :], row_gain, None, MULT)
 
@@ -279,7 +272,7 @@ def tile_list_syndrome_ring_decoder_kernel(
             nc.vector.tensor_tensor(
                 z_bf[:].rearrange("p (c i) t -> p c t i", i=2),
                 bent[:, :, b0 : b0 + c1 - c0].rearrange("p t (c i) -> p c t i", i=2),
-                hist[g][:, :, c0:c1].rearrange("p t (c i) -> p c t i", i=2),
+                scaled[g][:, :, c0:c1].rearrange("p t (c i) -> p c t i", i=2),
                 MULT,
             )
             return z_bf
@@ -321,30 +314,33 @@ def tile_list_syndrome_ring_decoder_kernel(
                     )
 
         pick_history(0)
+        pick_history(1)
+        w1_q.append(quantize("w1_1", w1_bf[1][:], BANK, at_tab1))
+        w3_second = round_w3(1, "w1_bf1")
         for t in range(PACK):
             project_page(0, t)
-        for g in range(2):
-            deal_w2(g)
-        pick_history(1)
-        w3_q.append(quantize("w3_1", w3_bf[1][:].rearrange("p c t -> p (c t)"), N, at_tab1))
         for t in range(PACK):
+            project_history(0, t)
+            apply_gain(0, t)
+        for t in (0, 1):
             project_page(1, t)
-        for g, t in [(0, 0), (0, 1), (0, 2), (0, 3), (1, 0), (1, 1)]:
-            project_history(g, t)
-            apply_gain(g, t)
+        w3_q.append(quantize("w3_1", w3_second, N, at_window5))
+        for t in (2, 3):
+            project_page(1, t)
         pieces = [[open_bank(0, HALF, n0, n0 + 2, "acc", 4) for n0 in (0, 2)]]
         add_prior(pieces[0], True)
         bent = [tanh_picked(0, h) for h in range(2)]
-        for t in (2, 3):
+        for t in range(PACK):
             project_history(1, t)
         pieces.append([open_bank(HALF, HALF + P, 0, 4, "bank0", 1)])
         pieces.append([open_bank(HALF + P, S, n0, n0 + 2, f"bank{1 + n0 // 2}", 1) for n0 in (0, 2)])
         add_prior(pieces[1], True)
         z_first = [product(0, bent[h], h * HALF, (h + 1) * HALF) for h in range(2)]
         mix(pieces[0], 0, quantize_z(0, z_first[0], 0, HALF), 0)
-        for t in (2, 3):
-            apply_gain(1, t)
+        apply_gain(1, 0)
         z_rest = quantize_z(0, z_first[1], HALF, S)
+        for t in (1, 2, 3):
+            apply_gain(1, t)
         mix(pieces[1], 0, z_rest, HALF)
         mix(pieces[2], 0, z_rest, HALF, True)
         add_prior(pieces[2], False)

@@ -44,13 +44,12 @@ def tile_list_syndrome_ring_decoder_kernel(
         idx_round = keep.tile([P, S // 16], U16, name="idx_round")
 
         at_fresh3 = 0
-        at_last_windows = [2048, 2048 + 8192]
-        at_dealt = [at + 3072 for at in at_last_windows]
-        at_bent = [at + 4096 for at in at_last_windows]
-        at_window5 = 2048 + 2 * 8192
-        at_late = at_window5 + 4096
-        at_tab1 = at_late + 8192
-        at_w3 = at_tab1 + 8192 + 512
+        at_late = 2048 + 1024
+        at_bent = [at_late - 1024, at_late + 3072]
+        at_dealt = [at_late + 2048, at_late + 7168]
+        at_window7 = at_late + 9216
+        at_tab = [at_window7 + 4096, at_window7 + 4096 + 8704]
+        at_w3 = at_tab[1] + 8192
 
         tab_s = sb("tab_s", [P, T], U8)
         w2_s_raw = sb("w2_s_raw", [P, H], U8)
@@ -87,7 +86,7 @@ def tile_list_syndrome_ring_decoder_kernel(
         fresh.append(placed("fresh3", [P, S], F32, at_fresh3))
         w1_raw = [sb("w1_raw0", [P, PACK, BANK], F32), placed("w1_raw1", [P, PACK, BANK], F32, at_late)]
         w3_raw = [sb("w3_raw0", [P, PACK, N], F32), placed("w3_raw1", [P, PACK, N], F32, at_w3)]
-        tab_w = [sb("tab_w0", [P, T], I32), placed("tab_w1", [P, T], I32, at_tab1)]
+        tab_w = [placed(f"tab_w{a}", [P, T], I32, at_tab[a]) for a in range(2)]
         w2_raw = sb("w2_raw", [P, 2, 2 * H], U8)
         w4_w = sb("w4_w", [P, 2, N], I32)
         gains = sb("gains", [P, 2 * PACK], F32)
@@ -101,8 +100,8 @@ def tile_list_syndrome_ring_decoder_kernel(
             nc.sync.dma_start(out=fresh[t][:], in_=xs_rows[:, t, :])
             nc.sync.dma_start(out=page[t][:], in_=base_rows[:, t, :])
 
-        def load_w3(g):
-            for t in range(PACK):
+        def load_w3(g, slots):
+            for t in slots:
                 nc.sync.dma_start(out=w3_raw[g][:, t, :], in_=w3_rows[g, t])
 
         def load_tab(a):
@@ -115,19 +114,22 @@ def tile_list_syndrome_ring_decoder_kernel(
         nc.vector.tensor_copy(v_s_rows[:], tab_s[:].indirect(idx_tab[:]))
         load_page(1)
         nc.sync.dma_start(out=w1_raw[0][:], in_=w1_rows[:, :, 0:BANK])
+        load_page(2)
+        load_w3(0, (0, 1))
+        load_page(3)
+        nc.sync.dma_start(out=w2_s_raw[0:32, :].bitcast(I32), in_=w2_scales.rearrange("a r c -> r a c").bitcast(I32))
+        nc.sync.dma_start(idx_round[:], offs3)
+        load_w3(0, (2, 3))
+        nc.sync.dma_start(out=w1_raw[1][:], in_=w1_rows[:, :, BANK : 2 * BANK])
+        load_tab(0)
         for g in range(2):
             nc.sync.dma_start(
                 out=gain_rows[PACK * g : PACK * (g + 1), :].rearrange("t (m e) -> t m e", e=4),
                 in_=gain.rearrange("(g m t e) -> g t m e", g=2, t=PACK, e=4)[g],
             )
-        nc.sync.dma_start(out=w2_s_raw[0:32, :].bitcast(I32), in_=w2_scales.rearrange("a r c -> r a c").bitcast(I32))
-        nc.sync.dma_start(idx_round[:], offs3)
-        load_page(2)
-        load_w3(0)
-        load_page(3)
         nc.sync.dma_start(out=w2_raw[:].bitcast(I32), in_=w2_words.rearrange("a p c -> p a c").bitcast(I32))
-        nc.sync.dma_start(out=w1_raw[1][:], in_=w1_rows[:, :, BANK : 2 * BANK])
-        load_tab(0)
+        load_tab(1)
+        load_w3(1, range(PACK))
 
         nc.gpsimd.tensor_copy(
             out=w2_s_rows[0:32, :].bitcast(I32).rearrange("p (b t m) -> p b t m", b=2, t=PACK),
@@ -135,14 +137,8 @@ def tile_list_syndrome_ring_decoder_kernel(
         )
         place_scale_rows(v_s_planes, v_s_rows)
         place_scale_rows(w2_s, w2_s_rows)
-        load_tab(1)
-        load_w3(1)
         nc.sync.dma_start(out=w4_w[:], in_=w4_words.rearrange("a p c i -> p a (c i)").bitcast(I32))
         load_scale_rows(w4_s, w4_scales)
-
-        gain_turned = psum.tile([P, BANK], F32, name="gain_turned", tag="bank3")
-        nc.tensor.transpose(gain_turned[:, 0:P], gain_rows[:], ident[:])
-        nc.scalar.copy(out=gains[:], in_=gain_turned[:, 0 : 2 * PACK])
 
         def quantize(name, grouped, width, scales_at=None):
             codes = sb(f"{name}_codes", [P, width], U32)
@@ -195,7 +191,6 @@ def tile_list_syndrome_ring_decoder_kernel(
         w3_first = round_w3(0, None)
         put_rounds(3)
         round_page(3)
-        w2_w = [deal_w2(g) for g in range(2)]
         round_w1(1)
         w1_q = [quantize("w1_0", w1_bf[0][:], BANK, at_fresh3)]
         w3_q = [quantize("w3_0", w3_first, N, at_fresh3 + 512)]
@@ -213,15 +208,15 @@ def tile_list_syndrome_ring_decoder_kernel(
         def pick_history(a):
             nc.vector.tensor_copy(v_w[a][:].bitcast(U32), tab_w[a][:].bitcast(U32).indirect(idx_tab[:]))
 
-        picked = [placed("picked0", [P, PACK, S], F32, at_tab1 + 512), sb("picked1", [P, PACK, S], F32)]
+        picked = [placed("picked0", [P, PACK, S], F32, at_tab[0] + 512), placed("picked1", [P, PACK, S], F32, at_tab[1])]
         hist = [sb(f"hist{g}", [P, PACK, S], F32) for g in range(2)]
         scaled = [placed("scaled0", [P, PACK, S], F32, at_w3), hist[1]]
 
         def project_page(g, t):
             if g == 0 and t < 2:
                 window = placed(f"rounds{g}{t}", [P, T2], F32, at_late + 4096 * t)
-            elif g == 1 and t > 0:
-                window = placed(f"rounds{g}{t}", [P, T2], F32, at_window5 if t == 1 else at_last_windows[t - 2])
+            elif g == 1 and t == 3:
+                window = placed(f"rounds{g}{t}", [P, T2], F32, at_window7)
             else:
                 window = sb(f"rounds{g}{t}", [P, T2], F32)
             cols = slice(t * P, (t + 1) * P)
@@ -314,19 +309,22 @@ def tile_list_syndrome_ring_decoder_kernel(
                     )
 
         pick_history(0)
-        pick_history(1)
-        w1_q.append(quantize("w1_1", w1_bf[1][:], BANK, at_tab1))
-        w3_second = round_w3(1, "w1_bf1")
+        w1_q.append(quantize("w1_1", w1_bf[1][:], BANK, at_tab[0]))
         for t in range(PACK):
             project_page(0, t)
+        w2_w = [deal_w2(g) for g in range(2)]
+        w3_second = round_w3(1, "w1_bf1")
+        pick_history(1)
+        for t in range(PACK):
+            project_page(1, t)
+        gain_turned = psum.tile([P, BANK], F32, name="gain_turned", tag="bank3")
+        nc.tensor.transpose(gain_turned[:, 0:P], gain_rows[:], ident[:])
+        nc.scalar.copy(out=gains[:], in_=gain_turned[:, 0 : 2 * PACK])
+
         for t in range(PACK):
             project_history(0, t)
             apply_gain(0, t)
-        for t in (0, 1):
-            project_page(1, t)
-        w3_q.append(quantize("w3_1", w3_second, N, at_window5))
-        for t in (2, 3):
-            project_page(1, t)
+        w3_q.append(quantize("w3_1", w3_second, N, at_window7))
         pieces = [[open_bank(0, HALF, n0, n0 + 2, "acc", 4) for n0 in (0, 2)]]
         add_prior(pieces[0], True)
         bent = [tanh_picked(0, h) for h in range(2)]

@@ -44,12 +44,12 @@ def tile_list_syndrome_ring_decoder_kernel(
         idx_round = keep.tile([P, S // 16], U16, name="idx_round")
 
         at_fresh3 = 0
-        at_late = 2048 + 1024
-        at_bent = [at_late - 1024, at_late + 3072]
-        at_dealt = [at_late + 2048, at_late + 7168]
-        at_window7 = at_late + 9216
-        at_tab = [at_window7 + 4096, at_window7 + 4096 + 8704]
-        at_w3 = at_tab[1] + 8192
+        at_late = 2048 + 2048
+        at_bent = [at_late - 2048, at_late + 6656]
+        at_dealt = [at_late + 1536, at_late + 7168]
+        at_window7 = at_late + 3072
+        at_tab = [at_bent[1] + 4096, at_bent[1] + 4096 + 8704]
+        at_w3 = at_tab[1] + 16384
 
         tab_s = sb("tab_s", [P, T], U8)
         w2_s_raw = sb("w2_s_raw", [P, H], U8)
@@ -84,8 +84,9 @@ def tile_list_syndrome_ring_decoder_kernel(
         page = [sb(f"page{t}", [P, T2], F32) for t in range(PACK)]
         fresh = [sb(f"fresh{t}", [P, S], F32) for t in range(PACK - 1)]
         fresh.append(placed("fresh3", [P, S], F32, at_fresh3))
-        w1_raw = [sb("w1_raw0", [P, PACK, BANK], F32), placed("w1_raw1", [P, PACK, BANK], F32, at_late)]
-        w3_raw = [sb("w3_raw0", [P, PACK, N], F32), placed("w3_raw1", [P, PACK, N], F32, at_w3)]
+        w1_first = sb("w1_first", [P, PACK, BANK], F32)
+        w1_second = [sb(f"w1_second{h}", [P, PACK, HALF], F32) for h in range(2)]
+        w3_raw = [placed("w3_raw0", [P, PACK, N], F32, at_late), placed("w3_raw1", [P, PACK, N], F32, at_w3)]
         tab_w = [placed(f"tab_w{a}", [P, T], I32, at_tab[a]) for a in range(2)]
         w2_raw = sb("w2_raw", [P, 2, 2 * H], U8)
         w4_w = sb("w4_w", [P, 2, N], I32)
@@ -100,8 +101,11 @@ def tile_list_syndrome_ring_decoder_kernel(
             nc.sync.dma_start(out=fresh[t][:], in_=xs_rows[:, t, :])
             nc.sync.dma_start(out=page[t][:], in_=base_rows[:, t, :])
 
-        def load_w3(g, slots):
-            for t in slots:
+        def load_w1_second(h):
+            nc.sync.dma_start(out=w1_second[h][:], in_=w1_rows[:, :, BANK + h * HALF : BANK + (h + 1) * HALF])
+
+        def load_w3(g):
+            for t in range(PACK):
                 nc.sync.dma_start(out=w3_raw[g][:, t, :], in_=w3_rows[g, t])
 
         def load_tab(a):
@@ -113,14 +117,14 @@ def tile_list_syndrome_ring_decoder_kernel(
         load_page(0)
         nc.vector.tensor_copy(v_s_rows[:], tab_s[:].indirect(idx_tab[:]))
         load_page(1)
-        nc.sync.dma_start(out=w1_raw[0][:], in_=w1_rows[:, :, 0:BANK])
         load_page(2)
-        load_w3(0, (0, 1))
+        nc.sync.dma_start(out=w1_first[:], in_=w1_rows[:, :, 0:BANK])
         load_page(3)
+        load_w1_second(0)
         nc.sync.dma_start(out=w2_s_raw[0:32, :].bitcast(I32), in_=w2_scales.rearrange("a r c -> r a c").bitcast(I32))
         nc.sync.dma_start(idx_round[:], offs3)
-        load_w3(0, (2, 3))
-        nc.sync.dma_start(out=w1_raw[1][:], in_=w1_rows[:, :, BANK : 2 * BANK])
+        load_w1_second(1)
+        load_w3(0)
         load_tab(0)
         for g in range(2):
             nc.sync.dma_start(
@@ -129,7 +133,6 @@ def tile_list_syndrome_ring_decoder_kernel(
             )
         nc.sync.dma_start(out=w2_raw[:].bitcast(I32), in_=w2_words.rearrange("a p c -> p a c").bitcast(I32))
         load_tab(1)
-        load_w3(1, range(PACK))
 
         nc.gpsimd.tensor_copy(
             out=w2_s_rows[0:32, :].bitcast(I32).rearrange("p (b t m) -> p b t m", b=2, t=PACK),
@@ -137,6 +140,7 @@ def tile_list_syndrome_ring_decoder_kernel(
         )
         place_scale_rows(v_s_planes, v_s_rows)
         place_scale_rows(w2_s, w2_s_rows)
+        load_w3(1)
         nc.sync.dma_start(out=w4_w[:], in_=w4_words.rearrange("a p c i -> p a (c i)").bitcast(I32))
         load_scale_rows(w4_s, w4_scales)
 
@@ -152,27 +156,34 @@ def tile_list_syndrome_ring_decoder_kernel(
         pairs = [sb(f"pairs{h}", [P, 2, BANK, 2], BF16) for h in range(2)]
         w1_bf = [sb(f"w1_bf{g}", [P, BANK * PACK], BF16) for g in range(2)]
 
-        def round_w1(g):
-            nc.scalar.copy(
-                out=w1_bf[g][:].rearrange("p (t m e j) -> p t m j e", t=PACK, e=4, j=PACK),
-                in_=w1_raw[g][:].rearrange("p j (m t e) -> p t m j e", t=PACK, e=4),
-            )
+        w3_first = sb("w3_bf0", [P, N, PACK], BF16)
 
-        def round_w3(g, tag):
-            grouped = sb(f"w3_bf{g}", [P, N, PACK], BF16, tag)
+        def round_w1_second(h):
+            for m0 in (0, 8):
+                nc.gpsimd.tensor_scalar(
+                    w1_bf[1][:].rearrange("p (t m e j) -> p m t e j", t=PACK, e=4, j=PACK)[:, 16 * h + m0 : 16 * h + m0 + 8],
+                    w1_second[h][:].rearrange("p j (m t e) -> p m t e j", t=PACK, e=4)[:, m0 : m0 + 8],
+                    1.0,
+                    0.0,
+                    MULT,
+                    ADD,
+                )
+
+        def round_w3_second():
+            grouped = sb("w3_bf1", [P, N, PACK], BF16, "w3_bf0")
             for c0 in range(0, N, P):
                 nc.gpsimd.tensor_scalar(
-                    grouped[:, c0 : c0 + P, :], w3_raw[g][:, :, c0 : c0 + P].rearrange("p t c -> p c t"), 1.0, 0.0, MULT, ADD
+                    grouped[:, c0 : c0 + P, :], w3_raw[1][:, :, c0 : c0 + P].rearrange("p t c -> p c t"), 1.0, 0.0, MULT, ADD
                 )
             return grouped[:].rearrange("p c t -> p (c t)")
 
-        def deal_w2(g):
-            dealt = placed(f"w2_w{g}", [P, 2, H], U8, at_dealt[g])
+        def deal_w2(dealt, g, t0, t1):
             nc.gpsimd.tensor_copy(
-                out=dealt[:].bitcast(I32).rearrange("p a (t m x) -> p a t m x", t=PACK, x=2),
-                in_=w2_raw[:, :, g * H : (g + 1) * H].bitcast(I32).rearrange("p a (m t x) -> p a t m x", t=PACK, x=2),
+                out=dealt.bitcast(I32).rearrange("p a (t m x) -> p a t m x", t=t1 - t0, x=2),
+                in_=w2_raw[:, :, g * H : (g + 1) * H].bitcast(I32).rearrange("p a (m t x) -> p a t m x", t=PACK, x=2)[
+                    :, :, t0:t1
+                ],
             )
-            return dealt
 
         def put_rounds(t):
             nc.vector.tensor_copy(page[t][:].indirect(idx_put[:]), fresh[t][:])
@@ -185,15 +196,26 @@ def tile_list_syndrome_ring_decoder_kernel(
         round_page(0)
         put_rounds(1)
         round_page(1)
-        round_w1(0)
+        for t in range(PACK):
+            nc.gpsimd.tensor_scalar(
+                w1_bf[0][:].rearrange("p (t m e j) -> p t m e j", t=PACK, e=4, j=PACK)[:, t],
+                w1_first[:].rearrange("p j (m t e) -> p t m e j", t=PACK, e=4)[:, t],
+                1.0,
+                0.0,
+                MULT,
+                ADD,
+            )
         put_rounds(2)
         round_page(2)
-        w3_first = round_w3(0, None)
+        round_w1_second(0)
         put_rounds(3)
         round_page(3)
-        round_w1(1)
-        w1_q = [quantize("w1_0", w1_bf[0][:], BANK, at_fresh3)]
-        w3_q = [quantize("w3_0", w3_first, N, at_fresh3 + 512)]
+        round_w1_second(1)
+        nc.scalar.copy(
+            out=w3_first[:].rearrange("p (c i) t -> p c t i", i=4),
+            in_=w3_raw[0][:].rearrange("p t (c i) -> p c t i", i=4),
+        )
+        w1_q = [quantize(f"w1_{g}", w1_bf[g][:], BANK, at_fresh3 + 512 * g) for g in range(2)]
 
         page_bf = [sb(f"page_bf{h}", [P, BANK * PACK], BF16) for h in range(2)]
         for h in range(2):
@@ -208,9 +230,13 @@ def tile_list_syndrome_ring_decoder_kernel(
         def pick_history(a):
             nc.vector.tensor_copy(v_w[a][:].bitcast(U32), tab_w[a][:].bitcast(U32).indirect(idx_tab[:]))
 
-        picked = [placed("picked0", [P, PACK, S], F32, at_tab[0] + 512), placed("picked1", [P, PACK, S], F32, at_tab[1])]
-        hist = [sb(f"hist{g}", [P, PACK, S], F32) for g in range(2)]
-        scaled = [placed("scaled0", [P, PACK, S], F32, at_w3), hist[1]]
+        picked_first = [
+            placed("picked00", [P, 2, S], F32, at_tab[0] + 512),
+            placed("picked01", [P, 2, S], F32, at_tab[1]),
+        ]
+        picked_second = placed("picked1", [P, PACK, S], F32, at_tab[1] + 4096)
+        hist = [sb("hist0", [P, PACK, S], F32, "w1_first"), sb("hist1", [P, PACK, S], F32)]
+        scaled = [placed(f"scaled{g}", [P, PACK, S], F32, at_w3 - 4096 + 8192 * g) for g in range(2)]
 
         def project_page(g, t):
             if g == 0 and t < 2:
@@ -232,11 +258,17 @@ def tile_list_syndrome_ring_decoder_kernel(
                     stop=True,
                 )
                 nc.scalar.copy(out=window[:, h * BANK : (h + 1) * BANK], in_=acc[:])
-            nc.vector.tensor_copy(picked[g][:, t, :], window[:].indirect(idx_round[:]))
+            into = picked_first[t // 2][:, t % 2, :] if g == 0 else picked_second[:, t, :]
+            nc.vector.tensor_copy(into, window[:].indirect(idx_round[:]))
 
         def tanh_picked(g, h):
             bent = placed(f"bent{g}{h}", [P, PACK, HALF], F32, at_bent[h])
-            nc.scalar.activation(out=bent[:], in_=picked[g][:, :, h * HALF : (h + 1) * HALF], func=ACT.Tanh)
+            cols = slice(h * HALF, (h + 1) * HALF)
+            if g == 0:
+                for u in range(2):
+                    nc.scalar.activation(out=bent[:, 2 * u : 2 * u + 2, :], in_=picked_first[u][:, :, cols], func=ACT.Tanh)
+            else:
+                nc.scalar.activation(out=bent[:], in_=picked_second[:, :, cols], func=ACT.Tanh)
             return bent
 
         def project_history(g, t):
@@ -245,7 +277,7 @@ def tile_list_syndrome_ring_decoder_kernel(
             for a in range(2):
                 nc.tensor.matmul_mx(
                     out=acc[:],
-                    lhsT=w2_w[g][:, a, 2 * t * P : 2 * (t + 1) * P].bitcast(FP4X4),
+                    lhsT=w2_slots[PACK * g + t][:, a, :].bitcast(FP4X4),
                     lhsT_scale=w2_s[:, a * H + c0 : a * H + c0 + P],
                     rhs=v_w[a][:].bitcast(FP8X4),
                     rhs_scale=v_s[a],
@@ -256,10 +288,10 @@ def tile_list_syndrome_ring_decoder_kernel(
 
         def apply_gain(g, t):
             row_gain = gains[:, PACK * g + t : PACK * g + t + 1]
-            if g == 0:
+            if g == 0 or t == 0:
                 nc.gpsimd.tensor_scalar(scaled[g][:, t, :], hist[g][:, t, :], row_gain, 0.0, MULT, ADD)
             else:
-                nc.vector.tensor_scalar(hist[g][:, t, :], hist[g][:, t, :], row_gain, None, MULT)
+                nc.vector.tensor_scalar(scaled[g][:, t, :], hist[g][:, t, :], row_gain, None, MULT)
 
         def product(g, bent, c0, c1):
             z_bf = sb(f"z_bf{g}_{c0}", [P, c1 - c0, PACK], BF16)
@@ -309,13 +341,21 @@ def tile_list_syndrome_ring_decoder_kernel(
                     )
 
         pick_history(0)
-        w1_q.append(quantize("w1_1", w1_bf[1][:], BANK, at_tab[0]))
-        for t in range(PACK):
+        w3_q = [quantize("w3_0", w3_first[:].rearrange("p c t -> p (c t)"), N, at_tab[0])]
+        for t in range(2):
             project_page(0, t)
-        w2_w = [deal_w2(g) for g in range(2)]
-        w3_second = round_w3(1, "w1_bf1")
         pick_history(1)
-        for t in range(PACK):
+        for t in range(2, PACK):
+            project_page(0, t)
+        w2_early = placed("w2_early", [P, 2, 5 * 2 * P], U8, at_dealt[0])
+        w2_late = placed("w2_late", [P, 2, 3 * 2 * P], U8, at_dealt[1])
+        deal_w2(w2_early[:, :, 0:H], 0, 0, 4)
+        deal_w2(w2_early[:, :, H : H + 2 * P], 1, 0, 1)
+        deal_w2(w2_late[:], 1, 1, 4)
+        w2_slots = [w2_early[:, :, 2 * P * u : 2 * P * (u + 1)] for u in range(5)]
+        w2_slots += [w2_late[:, :, 2 * P * u : 2 * P * (u + 1)] for u in range(3)]
+        w3_second = round_w3_second()
+        for t in range(PACK - 1):
             project_page(1, t)
         gain_turned = psum.tile([P, BANK], F32, name="gain_turned", tag="bank3")
         nc.tensor.transpose(gain_turned[:, 0:P], gain_rows[:], ident[:])
@@ -324,24 +364,27 @@ def tile_list_syndrome_ring_decoder_kernel(
         for t in range(PACK):
             project_history(0, t)
             apply_gain(0, t)
-        w3_q.append(quantize("w3_1", w3_second, N, at_window7))
-        pieces = [[open_bank(0, HALF, n0, n0 + 2, "acc", 4) for n0 in (0, 2)]]
-        add_prior(pieces[0], True)
+        project_page(1, 3)
+        project_history(1, 0)
+        apply_gain(1, 0)
+        w3_q.append(quantize("w3_1", w3_second, N, at_window7 + 1024))
+        pieces = [[open_bank(c0, c0 + P, 0, 4, "acc", 4)] for c0 in (0, P)]
+        add_prior(pieces[0] + pieces[1], True)
         bent = [tanh_picked(0, h) for h in range(2)]
-        for t in range(PACK):
+        for t in (1, 2, 3):
             project_history(1, t)
         pieces.append([open_bank(HALF, HALF + P, 0, 4, "bank0", 1)])
         pieces.append([open_bank(HALF + P, S, n0, n0 + 2, f"bank{1 + n0 // 2}", 1) for n0 in (0, 2)])
-        add_prior(pieces[1], True)
+        add_prior(pieces[2], True)
         z_first = [product(0, bent[h], h * HALF, (h + 1) * HALF) for h in range(2)]
-        mix(pieces[0], 0, quantize_z(0, z_first[0], 0, HALF), 0)
-        apply_gain(1, 0)
+        mix(pieces[0] + pieces[1], 0, quantize_z(0, z_first[0], 0, HALF), 0)
+        apply_gain(1, 1)
         z_rest = quantize_z(0, z_first[1], HALF, S)
-        for t in (1, 2, 3):
+        for t in (2, 3):
             apply_gain(1, t)
-        mix(pieces[1], 0, z_rest, HALF)
-        mix(pieces[2], 0, z_rest, HALF, True)
-        add_prior(pieces[2], False)
+        mix(pieces[2], 0, z_rest, HALF)
+        mix(pieces[3], 0, z_rest, HALF, True)
+        add_prior(pieces[3], False)
         bent = [tanh_picked(1, h) for h in range(2)]
         out_rows = out.rearrange("(n p) c -> p n c", p=P)
         for banks in pieces:
@@ -349,7 +392,7 @@ def tile_list_syndrome_ring_decoder_kernel(
             mix(banks, 1, quantize_z(1, product(1, bent[c0 // HALF], c0, c1), c0, c1), c0)
             for acc, c0, c1, n0, n1 in banks:
                 res = sb(f"res{c0}_{n0}", [P, n1 - n0, c1 - c0], F32)
-                if c0 >= HALF and n1 == 4:
+                if c1 == S and n1 == 4:
                     nc.vector.tensor_copy(out=res[:], in_=acc[:])
                 else:
                     nc.scalar.copy(out=res[:], in_=acc[:])

@@ -59,7 +59,8 @@ def tile_list_syndrome_ring_decoder_kernel(
         v_s_rows = sb("v_s_rows", [P, S], U8)
         v_s_planes = sb("v_s_planes", [P, 2 * S], U8)
         v_s = [v_s_planes[:, a * S : (a + 1) * S] for a in range(2)]
-        gain_rows = sb("gain_rows", [P, P], F32)
+        gain_raw = sb("gain_raw", [P, BANK], F32)
+        gain_rows = sb("gain_rows", [P, BANK], F32)
         nc.vector.memset(tab_s[32:64, :].bitcast(I32), 0)
         nc.vector.memset(tab_s[64:P, :].bitcast(I32), 0)
         nc.gpsimd.memset(gain_rows[:], 0.0)
@@ -117,20 +118,24 @@ def tile_list_syndrome_ring_decoder_kernel(
         load_page(0)
         nc.vector.tensor_copy(v_s_rows[:], tab_s[:].indirect(idx_tab[:]))
         load_page(1)
+        nc.sync.dma_start(out=w2_s_raw[0:32, :].bitcast(I32), in_=w2_scales.rearrange("a r c -> r a c").bitcast(I32))
+        nc.sync.dma_start(out=gain_raw[0:2, :], in_=gain.rearrange("(g r) -> g r", g=2))
+        nc.gpsimd.tensor_copy(
+            out=gain_rows[0:2, :].rearrange("g (t m e) -> g t m e", t=PACK, e=4),
+            in_=gain_raw[0:2, :].rearrange("g (m t e) -> g t m e", t=PACK, e=4),
+        )
+        gain_turned = psum.tile([P, PACK, P], F32, name="gain_turned", tag="bank3")
+        for t in range(PACK):
+            nc.tensor.transpose(gain_turned[:, t, :], gain_rows[:, t * P : (t + 1) * P], ident[:])
+        nc.scalar.copy(out=gains[:].rearrange("p (g t) -> p t g", g=2), in_=gain_turned[:, :, 0:2])
         load_page(2)
         nc.sync.dma_start(out=w1_first[:], in_=w1_rows[:, :, 0:BANK])
         load_page(3)
         load_w1_second(0)
-        nc.sync.dma_start(out=w2_s_raw[0:32, :].bitcast(I32), in_=w2_scales.rearrange("a r c -> r a c").bitcast(I32))
         nc.sync.dma_start(idx_round[:], offs3)
         load_w1_second(1)
         load_w3(0)
         load_tab(0)
-        for g in range(2):
-            nc.sync.dma_start(
-                out=gain_rows[PACK * g : PACK * (g + 1), :].rearrange("t (m e) -> t m e", e=4),
-                in_=gain.rearrange("(g m t e) -> g t m e", g=2, t=PACK, e=4)[g],
-            )
         nc.sync.dma_start(out=w2_raw[:].bitcast(I32), in_=w2_words.rearrange("a p c -> p a c").bitcast(I32))
         load_tab(1)
 
@@ -357,9 +362,6 @@ def tile_list_syndrome_ring_decoder_kernel(
         w3_second = round_w3_second()
         for t in range(PACK - 1):
             project_page(1, t)
-        gain_turned = psum.tile([P, BANK], F32, name="gain_turned", tag="bank3")
-        nc.tensor.transpose(gain_turned[:, 0:P], gain_rows[:], ident[:])
-        nc.scalar.copy(out=gains[:], in_=gain_turned[:, 0 : 2 * PACK])
 
         for t in range(PACK):
             project_history(0, t)

@@ -164,22 +164,18 @@ def tile_list_syndrome_ring_decoder_kernel(
         w3_first = sb("w3_bf0", [P, N, PACK], BF16)
 
         def round_w1_second(h):
-            for m0 in (0, 8):
-                nc.gpsimd.tensor_scalar(
-                    w1_bf[1][:].rearrange("p (t m e j) -> p m t e j", t=PACK, e=4, j=PACK)[:, 16 * h + m0 : 16 * h + m0 + 8],
-                    w1_second[h][:].rearrange("p j (m t e) -> p m t e j", t=PACK, e=4)[:, m0 : m0 + 8],
-                    1.0,
-                    0.0,
-                    MULT,
-                    ADD,
-                )
+            nc.gpsimd.tensor_scalar(
+                w1_bf[1][:].rearrange("p (t m e j) -> p m t e j", t=PACK, e=4, j=PACK)[:, 16 * h : 16 * h + 16],
+                w1_second[h][:].rearrange("p j (m t e) -> p m t e j", t=PACK, e=4),
+                1.0,
+                0.0,
+                MULT,
+                ADD,
+            )
 
         def round_w3_second():
             grouped = sb("w3_bf1", [P, N, PACK], BF16, "w3_bf0")
-            for c0 in range(0, N, P):
-                nc.gpsimd.tensor_scalar(
-                    grouped[:, c0 : c0 + P, :], w3_raw[1][:, :, c0 : c0 + P].rearrange("p t c -> p c t"), 1.0, 0.0, MULT, ADD
-                )
+            nc.gpsimd.tensor_scalar(grouped[:], w3_raw[1][:].rearrange("p t c -> p c t"), 1.0, 0.0, MULT, ADD)
             return grouped[:].rearrange("p c t -> p (c t)")
 
         def deal_w2(dealt, g, t0, t1):
@@ -201,15 +197,14 @@ def tile_list_syndrome_ring_decoder_kernel(
         round_page(0)
         put_rounds(1)
         round_page(1)
-        for t in range(PACK):
-            nc.gpsimd.tensor_scalar(
-                w1_bf[0][:].rearrange("p (t m e j) -> p t m e j", t=PACK, e=4, j=PACK)[:, t],
-                w1_first[:].rearrange("p j (m t e) -> p t m e j", t=PACK, e=4)[:, t],
-                1.0,
-                0.0,
-                MULT,
-                ADD,
-            )
+        nc.gpsimd.tensor_scalar(
+            w1_bf[0][:].rearrange("p (t m e j) -> p m t e j", t=PACK, e=4, j=PACK),
+            w1_first[:].rearrange("p j (m t e) -> p m t e j", t=PACK, e=4),
+            1.0,
+            0.0,
+            MULT,
+            ADD,
+        )
         put_rounds(2)
         round_page(2)
         round_w1_second(0)

from contextlib import ExitStack

import concourse.mybir as mybir
from concourse.masks import make_identity

K, K2, H, N, T, T2, S = 1024, 512, 1024, 512, 2048, 1024, 512
FLOPS = 2 * (K2 * H * T2 + K * H * S + H * N * S + K * N * S)

F32 = mybir.dt.float32
BF16 = mybir.dt.bfloat16
I32 = mybir.dt.int32
U32 = mybir.dt.uint32
U16 = mybir.dt.uint16
U8 = mybir.dt.uint8
FP8X4 = mybir.dt.float8_e4m3fn_x4
FP4X4 = mybir.dt.float4_e2m1fn_x4
ACT = mybir.ActivationFunctionType
MULT = mybir.AluOpType.mult
ADD = mybir.AluOpType.add

P = 128
PACK = 4
BANK = 512
HALF = S // 2


def tile_list_syndrome_ring_decoder_kernel(
    tc, tab_words, tab_scales, offs, offs2, offs3, base, xs, w1, w2_words, w2_scales, gain, w3, w4_words, w4_scales, out
):
    nc = tc.nc
    with ExitStack() as ctx:
        keep = ctx.enter_context(tc.tile_pool(name="keep", bufs=1))
        shared = ctx.enter_context(tc.tile_pool(name="shared", bufs=1))
        psum = ctx.enter_context(tc.psum_pool(name="psum", bufs=1))

        def sb(name, shape, dtype, tag=None):
            return keep.tile(shape, dtype, name=name, tag=tag or name, align_bytes=64)

        def placed(name, shape, dtype, offset):
            return shared.tile(shape, dtype, name=name, align_bytes=64, offset=offset)

        idx_tab = keep.tile([P, S // 16], U16, name="idx_tab")
        idx_put = keep.tile([P, S // 16], U16, name="idx_put")
        idx_round = keep.tile([P, S // 16], U16, name="idx_round")

        at_fresh3 = 0
        at_late = 2048 + 2048
        at_bent = [at_late - 2048, at_late + 6656]
        at_dealt = [at_late + 1536, at_late + 7168]
        at_window7 = at_late + 3072
        at_tab = [at_bent[1] + 4096, at_bent[1] + 4096 + 8704]
        at_w3 = at_tab[1] + 16384

        tab_s = sb("tab_s", [P, T], U8)
        w2_s_raw = sb("w2_s_raw", [P, H], U8)
        w2_s_rows = sb("w2_s_rows", [P, H], U8)
        w2_s = sb("w2_s", [P, 2 * H], U8)
        w4_s = sb("w4_s", [P, 2, N], U8)
        v_s_rows = sb("v_s_rows", [P, S], U8)
        v_s_planes = sb("v_s_planes", [P, 2 * S], U8)
        v_s = [v_s_planes[:, a * S : (a + 1) * S] for a in range(2)]
        gain_raw = sb("gain_raw", [P, BANK], F32)
        gain_rows = sb("gain_rows", [P, BANK], F32)
        nc.vector.memset(tab_s[32:64, :].bitcast(I32), 0)
        nc.vector.memset(tab_s[64:P, :].bitcast(I32), 0)
        nc.gpsimd.memset(gain_rows[:], 0.0)
        for plane in (v_s_planes, w2_s, w4_s):
            nc.gpsimd.memset(plane[:].bitcast(I32), 0)
        ident = sb("ident", [P, P], F32)
        make_identity(nc, ident[:])

        def load_scale_rows(planes, rows):
            for r in range(4):
                nc.sync.dma_start(
                    out=planes[r:P:32, :, :].bitcast(I32),
                    in_=rows.rearrange("a (q r) c -> r q a c", r=4)[r].bitcast(I32),
                )

        def place_scale_rows(planes, rows):
            for q in range(4):
                nc.sync.dma_start(
                    out=planes[32 * q : 32 * q + 4, :].bitcast(I32), in_=rows[8 * q : 8 * q + 8, :].bitcast(I32)
                )

        page = [sb(f"page{t}", [P, T2], F32) for t in range(PACK)]
        fresh = [sb(f"fresh{t}", [P, S], F32) for t in range(PACK - 1)]
        fresh.append(placed("fresh3", [P, S], F32, at_fresh3))
        w1_first = sb("w1_first", [P, PACK, BANK], F32)
        w1_second = [sb(f"w1_second{h}", [P, PACK, HALF], F32) for h in range(2)]
        w3_raw = [placed("w3_raw0", [P, PACK, N], F32, at_late), placed("w3_raw1", [P, PACK, N], F32, at_w3)]
        tab_w = [placed(f"tab_w{a}", [P, T], I32, at_tab[a]) for a in range(2)]
        w2_raw = sb("w2_raw", [P, 2, 2 * H], U8)
        w4_w = sb("w4_w", [P, 2, N], I32)
        gains = sb("gains", [P, 2 * PACK], F32)

        base_rows = base.rearrange("(p t) c -> p t c", t=PACK)
        xs_rows = xs.rearrange("(p t) c -> p t c", t=PACK)
        w1_rows = w1.rearrange("(p t) c -> p t c", t=PACK)
        w3_rows = w3.rearrange("(g m t e) n -> g t m e n", g=2, t=PACK, e=4)

        def load_page(t):
            nc.sync.dma_start(out=fresh[t][:], in_=xs_rows[:, t, :])
            nc.sync.dma_start(out=page[t][:], in_=base_rows[:, t, :])

        def load_w1_second(h):
            nc.sync.dma_start(out=w1_second[h][:], in_=w1_rows[:, :, BANK + h * HALF : BANK + (h + 1) * HALF])

        def load_w3(g):
            for t in range(PACK):
                nc.sync.dma_start(out=w3_raw[g][:, t, :], in_=w3_rows[g, t])

        def load_tab(a):
            nc.sync.dma_start(out=tab_w[a][:], in_=tab_words[a].rearrange("p c i -> p (c i)").bitcast(I32))

        nc.sync.dma_start(idx_tab[:], offs)
        nc.sync.dma_start(out=tab_s[0:32, :].bitcast(I32), in_=tab_scales.rearrange("a r c -> r a c").bitcast(I32))
        nc.sync.dma_start(idx_put[:], offs2)
        load_page(0)
        nc.vector.tensor_copy(v_s_rows[:], tab_s[:].indirect(idx_tab[:]))
        load_page(1)
        nc.sync.dma_start(out=w2_s_raw[0:32, :].bitcast(I32), in_=w2_scales.rearrange("a r c -> r a c").bitcast(I32))
        nc.sync.dma_start(out=gain_raw[0:2, :], in_=gain.rearrange("(g r) -> g r", g=2))
        nc.gpsimd.tensor_copy(
            out=gain_rows[0:2, :].rearrange("g (t m e) -> g t m e", t=PACK, e=4),
            in_=gain_raw[0:2, :].rearrange("g (m t e) -> g t m e", t=PACK, e=4),
        )
        gain_turned = psum.tile([P, PACK, P], F32, name="gain_turned", tag="bank3")
        for t in range(PACK):
            nc.tensor.transpose(gain_turned[:, t, :], gain_rows[:, t * P : (t + 1) * P], ident[:])
        nc.scalar.copy(out=gains[:].rearrange("p (g t) -> p t g", g=2), in_=gain_turned[:, :, 0:2])
        load_page(2)
        nc.sync.dma_start(out=w1_first[:], in_=w1_rows[:, :, 0:BANK])
        load_page(3)
        load_w1_second(0)
        nc.sync.dma_start(idx_round[:], offs3)
        load_w1_second(1)
        load_w3(0)
        load_tab(0)
        nc.sync.dma_start(out=w2_raw[:].bitcast(I32), in_=w2_words.rearrange("a p c -> p a c").bitcast(I32))
        load_tab(1)

        nc.gpsimd.tensor_copy(
            out=w2_s_rows[0:32, :].bitcast(I32).rearrange("p (b t m) -> p b t m", b=2, t=PACK),
            in_=w2_s_raw[0:32, :].bitcast(I32).rearrange("p (b m t) -> p b t m", b=2, t=PACK),
        )
        place_scale_rows(v_s_planes, v_s_rows)
        place_scale_rows(w2_s, w2_s_rows)
        load_w3(1)
        nc.sync.dma_start(out=w4_w[:], in_=w4_words.rearrange("a p c i -> p a (c i)").bitcast(I32))
        load_scale_rows(w4_s, w4_scales)

        def quantize(name, grouped, width, scales_at=None):
            codes = sb(f"{name}_codes", [P, width], U32)
            if scales_at is None:
                scales = sb(f"{name}_scales", [P, width], U8)
            else:
                scales = placed(f"{name}_scales", [P, width], U8, scales_at)
            nc.vector.quantize_mx(out=codes[:].bitcast(FP8X4), scales=scales[:], in_=grouped)
            return codes, scales

        pairs = [sb(f"pairs{h}", [P, 2, BANK, 2], BF16) for h in range(2)]
        w1_bf = [sb(f"w1_bf{g}", [P, BANK * PACK], BF16) for g in range(2)]

        w3_first = sb("w3_bf0", [P, N, PACK], BF16)

        def round_w1_second(h):
            nc.gpsimd.tensor_scalar(
                w1_bf[1][:].rearrange("p (t m e j) -> p m t e j", t=PACK, e=4, j=PACK)[:, 16 * h : 16 * h + 16],
                w1_second[h][:].rearrange("p j (m t e) -> p m t e j", t=PACK, e=4),
                1.0,
                0.0,
                MULT,
                ADD,
            )

        def round_w3_second():
            grouped = sb("w3_bf1", [P, N, PACK], BF16, "w3_bf0")
            nc.gpsimd.tensor_scalar(grouped[:], w3_raw[1][:].rearrange("p t c -> p c t"), 1.0, 0.0, MULT, ADD)
            return grouped[:].rearrange("p c t -> p (c t)")

        def deal_w2(dealt, g, t0, t1):
            nc.gpsimd.tensor_copy(
                out=dealt.bitcast(I32).rearrange("p a (t m x) -> p a t m x", t=t1 - t0, x=2),
                in_=w2_raw[:, :, g * H : (g + 1) * H].bitcast(I32).rearrange("p a (m t x) -> p a t m x", t=PACK, x=2)[
                    :, :, t0:t1
                ],
            )

        def put_rounds(t):
            nc.vector.tensor_copy(page[t][:].indirect(idx_put[:]), fresh[t][:])

        def round_page(t):
            for h in range(2):
                nc.scalar.copy(out=pairs[h][:, t // 2, :, t % 2], in_=page[t][:, h * BANK : (h + 1) * BANK])

        put_rounds(0)
        round_page(0)
        put_rounds(1)
        round_page(1)
        nc.gpsimd.tensor_scalar(
            w1_bf[0][:].rearrange("p (t m e j) -> p m t e j", t=PACK, e=4, j=PACK),
            w1_first[:].rearrange("p j (m t e) -> p m t e j", t=PACK, e=4),
            1.0,
            0.0,
            MULT,
            ADD,
        )
        put_rounds(2)
        round_page(2)
        round_w1_second(0)
        put_rounds(3)
        round_page(3)
        round_w1_second(1)
        nc.scalar.copy(
            out=w3_first[:].rearrange("p (c i) t -> p c t i", i=4),
            in_=w3_raw[0][:].rearrange("p t (c i) -> p c t i", i=4),
        )
        w1_q = [quantize(f"w1_{g}", w1_bf[g][:], BANK, at_fresh3 + 512 * g) for g in range(2)]

        page_bf = [sb(f"page_bf{h}", [P, BANK * PACK], BF16) for h in range(2)]
        for h in range(2):
            nc.vector.tensor_copy(
                out=page_bf[h][:].bitcast(F32).rearrange("p (c i u) -> p c u i", i=2, u=2),
                in_=pairs[h][:].rearrange("p u c x -> p u (c x)").bitcast(F32).rearrange("p u (c i) -> p c u i", i=2),
            )
        page_q = [quantize(f"page_{h}", page_bf[h][:], BANK) for h in range(2)]

        v_w = [sb(f"v_w{a}", [P, S], I32) for a in range(2)]

        def pick_history(a):
            nc.vector.tensor_copy(v_w[a][:].bitcast(U32), tab_w[a][:].bitcast(U32).indirect(idx_tab[:]))

        picked_first = [
            placed("picked00", [P, 2, S], F32, at_tab[0] + 512),
            placed("picked01", [P, 2, S], F32, at_tab[1]),
        ]
        picked_second = placed("picked1", [P, PACK, S], F32, at_tab[1] + 4096)
        hist = [sb("hist0", [P, PACK, S], F32, "w1_first"), sb("hist1", [P, PACK, S], F32)]
        scaled = [placed(f"scaled{g}", [P, PACK, S], F32, at_w3 - 4096 + 8192 * g) for g in range(2)]

        def project_page(g, t):
            if g == 0 and t < 2:
                window = placed(f"rounds{g}{t}", [P, T2], F32, at_late + 4096 * t)
            elif g == 1 and t == 3:
                window = placed(f"rounds{g}{t}", [P, T2], F32, at_window7)
            else:
                window = sb(f"rounds{g}{t}", [P, T2], F32)
            cols = slice(t * P, (t + 1) * P)
            for h in range(2):
                acc = psum.tile([P, BANK], F32, name="acc", tag="acc", bufs=4)
                nc.tensor.matmul_mx(
                    out=acc[:],
                    lhsT=w1_q[g][0][:, cols].bitcast(FP8X4),
                    lhsT_scale=w1_q[g][1][:, cols],
                    rhs=page_q[h][0][:].bitcast(FP8X4),
                    rhs_scale=page_q[h][1][:],
                    start=True,
                    stop=True,
                )
                nc.scalar.copy(out=window[:, h * BANK : (h + 1) * BANK], in_=acc[:])
            into = picked_first[t // 2][:, t % 2, :] if g == 0 else picked_second[:, t, :]
            nc.vector.tensor_copy(into, window[:].indirect(idx_round[:]))

        def tanh_picked(g, h):
            bent = placed(f"bent{g}{h}", [P, PACK, HALF], F32, at_bent[h])
            cols = slice(h * HALF, (h + 1) * HALF)
            if g == 0:
                for u in range(2):
                    nc.scalar.activation(out=bent[:, 2 * u : 2 * u + 2, :], in_=picked_first[u][:, :, cols], func=ACT.Tanh)
            else:
                nc.scalar.activation(out=bent[:], in_=picked_second[:, :, cols], func=ACT.Tanh)
            return bent

        def project_history(g, t):
            acc = psum.tile([P, BANK], F32, name=f"hist_acc{g}{t}", tag=f"bank{t}")
            c0 = g * BANK + t * P
            for a in range(2):
                nc.tensor.matmul_mx(
                    out=acc[:],
                    lhsT=w2_slots[PACK * g + t][:, a, :].bitcast(FP4X4),
                    lhsT_scale=w2_s[:, a * H + c0 : a * H + c0 + P],
                    rhs=v_w[a][:].bitcast(FP8X4),
                    rhs_scale=v_s[a],
                    start=(a == 0),
                    stop=(a == 1),
                )
            nc.scalar.activation(out=hist[g][:, t, :], in_=acc[:], func=ACT.Tanh)

        def apply_gain(g, t):
            row_gain = gains[:, PACK * g + t : PACK * g + t + 1]
            if g == 0 or t == 0:
                nc.gpsimd.tensor_scalar(scaled[g][:, t, :], hist[g][:, t, :], row_gain, 0.0, MULT, ADD)
            else:
                nc.vector.tensor_scalar(scaled[g][:, t, :], hist[g][:, t, :], row_gain, None, MULT)

        def product(g, bent, c0, c1):
            z_bf = sb(f"z_bf{g}_{c0}", [P, c1 - c0, PACK], BF16)
            b0 = c0 % HALF
            nc.vector.tensor_tensor(
                z_bf[:].rearrange("p (c i) t -> p c t i", i=2),
                bent[:, :, b0 : b0 + c1 - c0].rearrange("p t (c i) -> p c t i", i=2),
                scaled[g][:, :, c0:c1].rearrange("p t (c i) -> p c t i", i=2),
                MULT,
            )
            return z_bf

        def quantize_z(g, z_bf, c0, c1):
            return quantize(f"z_{g}_{c0}", z_bf[:].rearrange("p c t -> p (c t)"), c1 - c0)

        def open_bank(c0, c1, n0, n1, tag, bufs):
            acc = psum.tile([P, n1 - n0, c1 - c0], F32, name=f"out_acc{c0}_{n0}", tag=tag, bufs=bufs)
            return acc, c0, c1, n0, n1

        def add_prior(banks, first):
            for acc, c0, c1, n0, n1 in banks:
                for n in range(n0, n1):
                    cols = slice(n * P, (n + 1) * P)
                    for a in range(2):
                        nc.tensor.matmul_mx(
                            out=acc[:, n - n0, :],
                            lhsT=w4_w[:, a, cols].bitcast(FP8X4),
                            lhsT_scale=w4_s[:, a, cols],
                            rhs=v_w[a][:, c0:c1].bitcast(FP8X4),
                            rhs_scale=v_s[a][:, c0:c1],
                            start=(first and n == n0 and a == 0),
                            stop=False,
                        )

        def mix(banks, g, z, z0, first=False):
            for acc, c0, c1, n0, n1 in banks:
                for n in range(n0, n1):
                    cols = slice(n * P, (n + 1) * P)
                    nc.tensor.matmul_mx(
                        out=acc[:, n - n0, :],
                        lhsT=w3_q[g][0][:, cols].bitcast(FP8X4),
                        lhsT_scale=w3_q[g][1][:, cols],
                        rhs=z[0][:, c0 - z0 : c1 - z0].bitcast(FP8X4),
                        rhs_scale=z[1][:, c0 - z0 : c1 - z0],
                        start=(first and n == n0),
                        stop=(g == 1 and n == n1 - 1),
                    )

        pick_history(0)
        w3_q = [quantize("w3_0", w3_first[:].rearrange("p c t -> p (c t)"), N, at_tab[0])]
        for t in range(2):
            project_page(0, t)
        pick_history(1)
        for t in range(2, PACK):
            project_page(0, t)
        w2_early = placed("w2_early", [P, 2, 5 * 2 * P], U8, at_dealt[0])
        w2_late = placed("w2_late", [P, 2, 3 * 2 * P], U8, at_dealt[1])
        deal_w2(w2_early[:, :, 0:H], 0, 0, 4)
        deal_w2(w2_early[:, :, H : H + 2 * P], 1, 0, 1)
        deal_w2(w2_late[:], 1, 1, 4)
        w2_slots = [w2_early[:, :, 2 * P * u : 2 * P * (u + 1)] for u in range(5)]
        w2_slots += [w2_late[:, :, 2 * P * u : 2 * P * (u + 1)] for u in range(3)]
        w3_second = round_w3_second()
        for t in range(PACK - 1):
            project_page(1, t)

        for t in range(PACK):
            project_history(0, t)
            apply_gain(0, t)
        project_page(1, 3)
        project_history(1, 0)
        apply_gain(1, 0)
        w3_q.append(quantize("w3_1", w3_second, N, at_window7 + 1024))
        pieces = [[open_bank(c0, c0 + P, 0, 4, "acc", 4)] for c0 in (0, P)]
        add_prior(pieces[0] + pieces[1], True)
        bent = [tanh_picked(0, h) for h in range(2)]
        for t in (1, 2, 3):
            project_history(1, t)
        pieces.append([open_bank(HALF, HALF + P, 0, 4, "bank0", 1)])
        pieces.append([open_bank(HALF + P, S, n0, n0 + 2, f"bank{1 + n0 // 2}", 1) for n0 in (0, 2)])
        add_prior(pieces[2], True)
        z_first = [product(0, bent[h], h * HALF, (h + 1) * HALF) for h in range(2)]
        mix(pieces[0] + pieces[1], 0, quantize_z(0, z_first[0], 0, HALF), 0)
        apply_gain(1, 1)
        z_rest = quantize_z(0, z_first[1], HALF, S)
        for t in (2, 3):
            apply_gain(1, t)
        mix(pieces[2], 0, z_rest, HALF)
        mix(pieces[3], 0, z_rest, HALF, True)
        add_prior(pieces[3], False)
        bent = [tanh_picked(1, h) for h in range(2)]
        out_rows = out.rearrange("(n p) c -> p n c", p=P)
        for banks in pieces:
            c0, c1 = banks[0][1], banks[0][2]
            mix(banks, 1, quantize_z(1, product(1, bent[c0 // HALF], c0, c1), c0, c1), c0)
            for acc, c0, c1, n0, n1 in banks:
                res = sb(f"res{c0}_{n0}", [P, n1 - n0, c1 - c0], F32)
                if c1 == S and n1 == 4:
                    nc.vector.tensor_copy(out=res[:], in_=acc[:])
                else:
                    nc.scalar.copy(out=res[:], in_=acc[:])
                nc.sync.dma_start(out=out_rows[:, n0:n1, c0:c1], in_=res[:])
